import numpy as np
import ml_dtypes


def mxq(x, axis, fmt="e4m3"):
    dtype, down = {"e4m3": (ml_dtypes.float8_e4m3fn, 7), "e5m2": (ml_dtypes.float8_e5m2, 14)}[fmt]
    v = np.moveaxis(np.asarray(x, np.float32).astype(ml_dtypes.bfloat16).astype(np.float64), axis, -1)
    blocks = v.reshape(v.shape[:-1] + (-1, 32))
    amax = np.abs(blocks).max(-1, keepdims=True)
    byte = np.maximum(np.where(amax > 0, np.frexp(amax)[1] - 1 + 127, 0) - down, 1)
    scale = np.exp2(byte - 127.0)
    codes = (blocks / scale).astype(np.float32).astype(dtype).astype(np.float64)
    return np.moveaxis((codes * scale).reshape(v.shape), -1, axis)


WIDE = False


def mx_kscale(k):
    if not WIDE:
        return np.ones(k)
    levels = np.array([24, -24, 12, -12, 0])
    if k % 512:
        return np.exp2(np.random.permutation(np.resize(levels, k // 32))).repeat(32)
    a = np.empty((k // 512, 16))
    for p in range(k // 512):
        a[p, :8] = np.random.permutation(np.resize(levels, 8))
        for g in range(8):
            far = levels[np.abs(levels - a[p, g]) >= 10]
            a[p, g + 8] = far[np.random.randint(len(far))]
    return np.exp2(a.ravel()).repeat(32)


def f64(x):
    return np.asarray(x).astype(np.float64)


def striped(idx):
    return np.tile(idx.reshape(-1, 16).T, (8, 1)).astype(np.uint16)


def unstriped(offs):
    return offs[:16].T.reshape(-1).astype(np.int64)


E2M1 = np.array([0.0, 0.5, 1.0, 1.5, 2.0, 3.0, 4.0, 6.0, -0.0, -0.5, -1.0, -1.5, -2.0, -3.0, -4.0, -6.0])


def pack_weight(w, fmt):
    k, n = w.shape
    w = f64(np.asarray(w, np.float32).astype(ml_dtypes.bfloat16)).reshape(k // 32, 32, n)
    amax = np.abs(w).max(1)
    if fmt == "e4m3":
        byte = np.frexp(amax)[1] - 1 + 127 - 7
    else:
        mant, ex = np.frexp(amax / 6.0)
        byte = np.where(mant > 0.5, ex, ex - 1) + 127
    byte = np.clip(np.where(amax > 0, byte, 1), 1, 254)
    scaled = (w * np.exp2(127.0 - byte)[:, None, :]).reshape(k, n).astype(np.float32)
    by_word = np.ascontiguousarray(scaled.reshape(k // 512, 128, 4, n).transpose(0, 1, 3, 2))
    if fmt == "e4m3":
        words = by_word.astype(ml_dtypes.float8_e4m3fn).view(np.uint8)
    else:
        c = by_word.astype(ml_dtypes.float4_e2m1fn).view(np.uint8) & 0xF
        words = (c[..., 0::2] | (c[..., 1::2] << 4)).reshape(k // 512, 128, 2 * n)
    return np.ascontiguousarray(words), np.ascontiguousarray(byte.astype(np.uint8).reshape(k // 512, 16, n))


def unpack_weight(words, scales, fmt):
    g, _, n = scales.shape
    words = np.ascontiguousarray(words).reshape(g, 128, n, -1)
    if fmt == "e4m3":
        vals = words.view(ml_dtypes.float8_e4m3fn).astype(np.float64)
    else:
        nib = np.empty((g, 128, n, 4), np.uint8)
        nib[..., 0::2] = words & 0xF
        nib[..., 1::2] = words >> 4
        vals = E2M1[nib]
    vals = vals * np.repeat(np.exp2(scales.astype(np.float64) - 127.0), 8, axis=1)[..., None]
    return vals.transpose(0, 1, 3, 2).reshape(g * 512, n)


def pack_table4(v):
    words, scales = pack_weight(v, "e2m1")
    g, t = words.shape[0] // 2, v.shape[1]
    return np.ascontiguousarray(words.reshape(g, 2, 128, t, 2).transpose(0, 2, 3, 1, 4).reshape(g, 128, t, 4)), scales


def unpack_table4(words, scales):
    g, _, t, _ = words.shape
    return unpack_weight(words.reshape(g, 128, t, 2, 2).transpose(0, 3, 1, 2, 4).reshape(2 * g, 128, 2 * t), scales, "e2m1")


def planes(y):
    n, m = y.shape
    v = y.astype(np.float32).astype(ml_dtypes.bfloat16).astype(np.float64).reshape(n // 32, 32, m)
    top = np.abs(v).max(1)
    byte = np.clip(np.where(top > 0, np.frexp(top)[1] - 1 + 127 - 7, 1), 1, 254)
    codes = (v * np.exp2(127.0 - byte)[:, None, :]).reshape(n, m).astype(np.float32).astype(ml_dtypes.float8_e4m3fn).view(np.uint8)
    words = codes.reshape(n // 512, 128, 4, m).transpose(0, 1, 3, 2)
    return np.ascontiguousarray(words), np.ascontiguousarray(byte.astype(np.uint8).reshape(n // 512, 16, m))


def gelu(f):
    return 0.5 * f * (1.0 + np.tanh(np.sqrt(2.0 / np.pi) * (f + 0.044715 * f**3)))


K, R, N, T, J = 1024, 512, 512, 2048, 1024


def setup_inputs():
    n = np.random.standard_normal
    s = mx_kscale(K)[:, None]
    u = mx_kscale(R)[:, None]
    wd = n((R, N)) / np.sqrt(R) / u
    wd4 = pack_weight(wd, "e2m1")
    wdrest = wd - unpack_weight(*wd4, "e2m1")
    p_tab = pack_table4(n((K, T)) * s)
    p_wd8 = pack_weight(wdrest, "e4m3")
    return {
        "tab_words": p_tab[0],
        "tab_scales": p_tab[1],
        "ws": (n((K, R)) / np.sqrt(2 * K) / s).astype(np.float32),
        "wt": (n((K, R)) / np.sqrt(2 * K) / s).astype(np.float32),
        "sm": (np.random.uniform(0.5, 2.0, R) * u[:, 0]).astype(np.float32),
        "wd4_words": wd4[0],
        "wd4_scales": wd4[1],
        "wd8_words": p_wd8[0],
        "wd8_scales": p_wd8[1],
        "rT": (n((N, T))).astype(np.float32),
        "wgo": np.tile(np.random.uniform(0.5, 2.0, J), (128, 1)).astype(np.float32),
        "offs": striped(np.random.permutation(T)[:J]),
        "offs2": striped(np.random.permutation(T)[:J]),
    }


def reference(tab_words, tab_scales, ws, wt, sm, wd4_words, wd4_scales, wd8_words, wd8_scales, rT, wgo, offs, offs2):
    idx = unstriped(offs)
    idx2 = unstriped(offs2)
    tab_ = unpack_table4(tab_words, tab_scales)[:, idx]
    tabb_ = unpack_table4(tab_words, tab_scales)[:, idx2]
    ws_ = mxq(f64(ws), 0, "e4m3")
    wt_ = mxq(f64(wt), 0, "e4m3")
    a = ws_.T @ tab_ + wt_.T @ tabb_
    h = f64(sm)[:, None] * gelu(a)
    h_ = mxq(h, 0, "e4m3")
    wd4_ = unpack_weight(wd4_words, wd4_scales, "e2m1")
    wd8_ = unpack_weight(wd8_words, wd8_scales, "e4m3")
    y = wd4_.T @ h_ + wd8_.T @ h_
    out = np.zeros((N, T))
    out[:, idx2] = f64(wgo)[0] * (y + f64(rT)[:, idx2])
    return (out,) + planes(out)

@@ -1,0 +1,331 @@
+from contextlib import ExitStack
+
+import concourse.mybir as mybir
+from concourse.masks import make_identity
+
+K, R, N, T, J = 1024, 512, 512, 2048, 1024
+FLOPS = 2 * J * (2 * K * R + 2 * R * N)
+
+F32 = mybir.dt.float32
+BF16 = mybir.dt.bfloat16
+I32 = mybir.dt.int32
+U32 = mybir.dt.uint32
+U16 = mybir.dt.uint16
+U8 = mybir.dt.uint8
+FP8X4 = mybir.dt.float8_e4m3fn_x4
+FP4X4 = mybir.dt.float4_e2m1fn_x4
+MULT = mybir.AluOpType.mult
+ADD = mybir.AluOpType.add
+GELU = mybir.ActivationFunctionType.Gelu_apprx_tanh
+COPY = mybir.ActivationFunctionType.Copy
+
+P = 128
+PACK = 4
+HALF = J // 2
+QUARTER = J // 4
+PER_COL = 16
+
+VECTOR_WIDTHS = (512, 512, 128)
+SCALAR_WIDTHS = (256, 256, 256, 128)
+STORE_CUTS = (0, 512, 1024, 1664, 2048)
+
+
+def tile_list_msg_gelu_res_resLP_kernel(
+    tc, tab_words, tab_scales, ws, wt, sm, wd4_words, wd4_scales, wd8_words, wd8_scales, rT, wgo, offs, offs2,
+    out_0, out_1, out_2,
+):
+    nc = tc.nc
+    with ExitStack() as ctx:
+        sb = ctx.enter_context(tc.tile_pool(name="sb", bufs=1))
+        ps = ctx.enter_context(tc.psum_pool(name="ps", bufs=1))
+
+        def sbuf(shape, dtype, name, slot=None):
+            return sb.tile(shape, dtype, name=name, tag=slot or name, align_bytes=64)
+
+        def bank(shape, name, index):
+            return ps.tile(shape, F32, name=name, tag="bank%d" % index)
+
+        def entries(list_tile, first, count):
+            return list_tile[:, first // PER_COL : (first + count) // PER_COL]
+
+        tab_sc = sbuf([P, T], U8, "tab_sc")
+        nc.gpsimd.memset(tab_sc[:].bitcast(I32), 0)
+        wd_sc = sbuf([P, 2 * N], U8, "wd_sc")
+        nc.vector.memset(wd_sc[:].bitcast(I32), 0)
+        moved_sc = [sbuf([P, 2 * HALF], U8, "moved_sc%d" % h) for h in range(2)]
+        for h in range(2):
+            nc.vector.memset(moved_sc[h][:].bitcast(I32), 0)
+        page = [sbuf([P, T], F32, "page%d" % t) for t in range(PACK)]
+        for t in range(PACK):
+            nc.vector.memset(page[t][:], 0.0)
+
+        lists = [sbuf([P, J // PER_COL], U16, "list%d" % s) for s in range(2)]
+        tab = sbuf([P, T], I32, "tab")
+        nc.sync.dma_start(lists[0][:], offs)
+        nc.sync.dma_start(lists[1][:], offs2)
+        sm_sb = sbuf([P, PACK], F32, "sm_sb")
+        nc.sync.dma_start(sm_sb[:], sm.rearrange("(p t) -> p t", t=PACK))
+        wd4 = sbuf([P, 2 * N], U8, "wd4")
+        nc.sync.dma_start(wd4[:].bitcast(I32), wd4_words[0].bitcast(I32))
+        nc.sync.dma_start(tab[:], tab_words[0].rearrange("p t i -> p (t i)").bitcast(I32))
+        for q in range(4):
+            nc.scalar.dma_start(
+                tab_sc[32 * q : 32 * q + 8, :].bitcast(I32), tab_scales[:, 4 * q : 4 * q + 4, :].bitcast(I32)
+            )
+        w_raw = []
+        for s, w in enumerate((ws, wt)):
+            for a in range(2):
+                raw = sbuf([P, PACK, R], F32, "w_raw%d%d" % (s, a))
+                nc.sync.dma_start(raw[:], w[512 * a : 512 * (a + 1), :].rearrange("(p j) r -> p j r", j=PACK))
+                w_raw.append(raw)
+        wgo_sb = sbuf([P, J], F32, "wgo_sb")
+        nc.sync.dma_start(wgo_sb[:], wgo)
+        r_rows = rT.rearrange("(p t) c -> p t c", t=PACK)
+        r_sb = [sbuf([P, T], F32, "r_sb%d" % t) for t in range(PACK)]
+        nc.sync.dma_start(r_sb[0][:], r_rows[:, 0, :])
+        wd8 = sbuf([P, N], I32, "wd8")
+        nc.sync.dma_start(wd8[:], wd8_words[0].rearrange("p n i -> p (n i)").bitcast(I32))
+        for t in range(1, PACK):
+            nc.sync.dma_start(r_sb[t][:], r_rows[:, t, :])
+        for i, scales in enumerate((wd4_scales, wd8_scales)):
+            for q in range(4):
+                nc.gpsimd.dma_start(
+                    wd_sc[32 * q : 32 * q + 4, N * i : N * (i + 1)].bitcast(I32),
+                    scales[0, 4 * q : 4 * q + 4, :].bitcast(I32),
+                )
+        ident = sbuf([P, P], F32, "ident")
+        make_identity(nc, ident[:])
+
+        picked_sc = [None, None]
+        parted = {}
+
+        def pick_words(s, h, slot=None):
+            words = sbuf([P, HALF], U32, "words%d%d" % (s, h), slot)
+            nc.vector.tensor_copy(words[:], tab[:].bitcast(U32).indirect(entries(lists[s], HALF * h, HALF)))
+            return words
+
+        def part_words(s, h, words):
+            both = sbuf([P, 2 * 2 * HALF], U8, "parted%d%d" % (s, h))
+            nc.vector.tensor_copy(
+                both[:].bitcast(U16).rearrange("p (d j) -> p d j", d=2),
+                words[:].bitcast(U16).rearrange("p (j d) -> p d j", d=2),
+            )
+            parted[s, h] = both
+
+        def pick_scales(h, slot=None):
+            picked = sbuf([P, 2 * HALF], U8, "picked_sc%d" % h, slot)
+            for s in range(2):
+                nc.vector.tensor_copy(
+                    picked[:, HALF * s : HALF * (s + 1)], tab_sc[:].indirect(entries(lists[s], HALF * h, HALF))
+                )
+            nc.gpsimd.dma_start(moved_sc[h][0:100, :].bitcast(I32), picked[4:104, :].bitcast(I32))
+            picked_sc[h] = picked
+
+        w_codes, w_scales = [], []
+
+        def quantise_weight(i):
+            grouped = sbuf([P, PACK * R], BF16, "w_grouped%d" % i)
+            nc.scalar.copy(
+                grouped[:].rearrange("p (t m j) -> p m j t", t=PACK, j=PACK),
+                w_raw[i][:].rearrange("p j (m t) -> p m j t", t=PACK),
+            )
+            codes = sbuf([P, R], U32, "w_codes%d" % i)
+            scales = sbuf([P, R], U8, "w_scales%d" % i)
+            nc.vector.quantize_mx(out=codes[:].bitcast(FP8X4), scales=scales[:], in_=grouped[:])
+            w_codes.append(codes)
+            w_scales.append(scales)
+
+        acc = {}
+
+        def first_layer_pass(h, i):
+            s, a = divmod(i, 2)
+            plane = (picked_sc, moved_sc)[a][h]
+            for t in range(PACK):
+                if i == 0:
+                    acc[h, t] = bank([P, HALF], "acc%d%d" % (h, t), PACK * h + t)
+                nc.tensor.matmul_mx(
+                    out=acc[h, t][:],
+                    lhsT=w_codes[i][:, P * t : P * (t + 1)].bitcast(FP8X4),
+                    lhsT_scale=w_scales[i][:, P * t : P * (t + 1)],
+                    rhs=parted[s, h][:, 2 * HALF * a : 2 * HALF * (a + 1)].bitcast(FP4X4),
+                    rhs_scale=plane[:, HALF * s : HALF * (s + 1)],
+                    start=(i == 0),
+                    stop=(i == 3),
+                )
+
+        pick_scales(0)
+        first = [pick_words(s, 0) for s in range(2)]
+        for s in range(2):
+            part_words(s, 0, first[s])
+        quantise_weight(0)
+        first_layer_pass(0, 0)
+        part_words(0, 1, pick_words(0, 1, "w_grouped0"))
+        quantise_weight(1)
+        first_layer_pass(0, 1)
+        pick_scales(1, "w_grouped1")
+        quantise_weight(2)
+        first_layer_pass(0, 2)
+        late_words = pick_words(1, 1, "w_grouped2")
+        quantise_weight(3)
+        first_layer_pass(0, 3)
+        part_words(1, 1, late_words)
+
+        wgo_col = sbuf([P, J // P], F32, "wgo_col")
+        for g in range(2):
+            turned = bank([P, PACK, P], "wgo_turned%d" % g, PACK + g)
+            for b in range(PACK):
+                first_edge = P * (PACK * g + b)
+                nc.tensor.transpose(turned[:, b, :], wgo_sb[:, first_edge : first_edge + P], ident[:])
+            nc.scalar.copy(wgo_col[:, PACK * g : PACK * (g + 1)], turned[:, :, 0])
+
+        for i in range(4):
+            first_layer_pass(1, i)
+
+        rw = {}
+
+        def pick_residual(t, h, out):
+            nc.vector.tensor_tensor(
+                out, r_sb[t][:].indirect(entries(lists[1], HALF * h, HALF)), wgo_sb[:, HALF * h : HALF * (h + 1)], MULT
+            )
+            rw[t, h] = out
+
+        for t in range(PACK):
+            pick_residual(t, 0, sbuf([P, HALF], F32, "rw%d" % t)[:])
+
+        h_codes, h_scales, z = {}, {}, {}
+
+        def hidden(q):
+            h, c = divmod(q, 2)
+            cols = slice(QUARTER * c, QUARTER * (c + 1))
+            act = sbuf([P, PACK, QUARTER], F32, "act%d" % q, "act%d" % (q % 2))
+            scaled = sbuf([P, PACK, QUARTER], BF16, "scaled%d" % q, "scaled%d" % (q % 2))
+            for t in range(PACK):
+                nc.scalar.activation(act[:, t, :], acc[h, t][:, cols], GELU)
+            for t in range(PACK):
+                nc.scalar.activation(scaled[:, t, :], act[:, t, :], COPY, scale=sm_sb[:, t : t + 1])
+            grouped = sbuf([P, PACK * QUARTER], BF16, "h_grouped%d" % q)
+            nc.scalar.copy(
+                grouped[:].rearrange("p (c i t) -> p c t i", i=4, t=PACK),
+                scaled[:].rearrange("p t (c i) -> p c t i", i=4),
+            )
+            h_codes[q] = sbuf([P, QUARTER], U32, "h_codes%d" % q)
+            h_scales[q] = sbuf([P, QUARTER], U8, "h_scales%d" % q)
+            nc.vector.quantize_mx(out=h_codes[q][:].bitcast(FP8X4), scales=h_scales[q][:], in_=grouped[:])
+
+        def late_residuals(q):
+            pair = sbuf([P, 2, HALF], F32, "rw_late%d" % q, "h_grouped%d" % q)
+            for i in range(2):
+                pick_residual(2 * q + i, 1, pair[:, i, :])
+
+        def message(q):
+            z[q] = sbuf([P, PACK, QUARTER], F32, "z%d" % q)
+            y_sb = []
+            for b in range(2):
+                cols = slice(P * b, P * (b + 1))
+                y_ps = bank([P, N], "y_ps%d%d" % (q, b), b)
+                for i, (words, fmt) in enumerate(((wd4, FP4X4), (wd8, FP8X4))):
+                    nc.tensor.matmul_mx(
+                        out=y_ps[:],
+                        lhsT=h_codes[q][:, cols].bitcast(FP8X4),
+                        lhsT_scale=h_scales[q][:, cols],
+                        rhs=words[:].bitcast(fmt),
+                        rhs_scale=wd_sc[:, N * i : N * (i + 1)],
+                        start=(i == 0),
+                        stop=(i == 1),
+                    )
+                weighted = sbuf([P, PACK, P], F32, "y_sb%d%d" % (q, b), "y_sb%d%d" % (q % 2, b))
+                nc.scalar.activation(
+                    weighted[:],
+                    y_ps[:].rearrange("j (p t) -> j t p", t=PACK),
+                    COPY,
+                    scale=wgo_col[:, 2 * q + b : 2 * q + b + 1],
+                )
+                y_sb.append(weighted)
+            for b in range(2):
+                z_ps = bank([P, PACK, P], "z_ps%d%d" % (q, b), 2 + b)
+                for t in range(PACK):
+                    nc.tensor.transpose(z_ps[:, t, :], y_sb[b][:, t, :], ident[:])
+                nc.scalar.copy(z[q][:, :, P * b : P * (b + 1)], z_ps[:])
+
+        def scatter(q, t):
+            h, c = divmod(q, 2)
+            nc.vector.tensor_tensor(
+                page[t][:].indirect(entries(lists[1], QUARTER * q, QUARTER)),
+                z[q][:, t, :],
+                rw[t, h][:, QUARTER * c : QUARTER * (c + 1)],
+                ADD,
+            )
+
+        hidden(0)
+        late_residuals(0)
+        hidden(1)
+        late_residuals(1)
+        message(0)
+        for t in range(PACK):
+            scatter(0, t)
+        hidden(2)
+        message(1)
+        for t in range(PACK - 1):
+            scatter(1, t)
+        hidden(3)
+        message(2)
+        for t in range(PACK - 1):
+            scatter(2, t)
+        message(3)
+
+        out_rows = out_0.rearrange("(p t) c -> p t c", t=PACK)
+        split = sum(VECTOR_WIDTHS)
+        rounded = [
+            sbuf([P, PACK, split], BF16, "rounded0", "w_raw00"),
+            sbuf([P, PACK, T - split], BF16, "rounded1", "w_raw01"),
+        ]
+        for t in range(PACK - 1):
+            scatter(3, t)
+            nc.sync.dma_start(out_rows[:, t, :], page[t][:])
+            nc.scalar.copy(rounded[0][:, t, :], page[t][:, 0:split])
+            nc.scalar.copy(rounded[1][:, t, :], page[t][:, split:T])
+        last = PACK - 1
+        for q in (3, 1, 2):
+            scatter(q, last)
+        nc.sync.dma_start(out_rows[:, last, :], page[last][:])
+
+        codes = sbuf([P, T], I32, "out_codes")
+        scales = sbuf([P, T], U8, "out_scales")
+        free_slots = ["r_sb0", "r_sb1", "r_sb2", "r_sb3", "w_raw10", "w_raw11", "tab"]
+
+        def group(copy, source, source_first, first, width, n):
+            cols = slice(first - source_first, first - source_first + width)
+            copy(source[:, last, cols], page[last][:, first : first + width])
+            grouped = sbuf([P, PACK * width], BF16, "out_grouped%d" % n, free_slots[n])
+            copy(
+                grouped[:].rearrange("p (c i t) -> p c t i", i=4, t=PACK),
+                source[:, :, cols].rearrange("p t (c i) -> p c t i", i=4),
+            )
+            return grouped
+
+        def quantise_out(grouped, first, width):
+            nc.vector.quantize_mx(
+                out=codes[:, first : first + width].bitcast(FP8X4), scales=scales[:, first : first + width], in_=grouped[:]
+            )
+
+        by_scalar = []
+        first_col = split
+        for n, width in enumerate(SCALAR_WIDTHS):
+            by_scalar.append((group(nc.scalar.copy, rounded[1], split, first_col, width, len(VECTOR_WIDTHS) + n), first_col, width))
+            first_col = first_col + width
+        first_col = 0
+        waiting = []
+        for n, width in enumerate(VECTOR_WIDTHS):
+            grouped = group(nc.vector.tensor_copy, rounded[0], 0, first_col, width, n)
+            for item in waiting:
+                quantise_out(*item)
+            waiting = [by_scalar[n], (grouped, first_col, width)]
+            first_col = first_col + width
+        for item in waiting + by_scalar[len(VECTOR_WIDTHS) :]:
+            quantise_out(*item)
+
+        words_out = out_1[0].rearrange("p t i -> p (t i)").bitcast(I32)
+        for lo, hi in zip(STORE_CUTS, STORE_CUTS[1:]):
+            nc.sync.dma_start(words_out[:, lo:hi], codes[:, lo:hi])
+        for q in range(4):
+            nc.scalar.dma_start(out_2[0, 4 * q : 4 * q + 4, :].bitcast(I32), scales[32 * q : 32 * q + 4, :].bitcast(I32))

@@ -27,7 +27,7 @@ PER_COL = 16
 
 VECTOR_WIDTHS = (512, 512, 128)
 SCALAR_WIDTHS = (256, 256, 256, 128)
-STORE_CUTS = (0, 512, 1024, 1664, 2048)
+STORE_CUTS = (0, 512, 1152, 1664, 2048)
 
 
 def tile_list_msg_gelu_res_resLP_kernel(
@@ -50,51 +50,45 @@ def tile_list_msg_gelu_res_resLP_kernel(
 
         tab_sc = sbuf([P, T], U8, "tab_sc")
         nc.gpsimd.memset(tab_sc[:].bitcast(I32), 0)
+        ident = sbuf([P, P], F32, "ident")
+        make_identity(nc, ident[:])
         wd_sc = sbuf([P, 2 * N], U8, "wd_sc")
         nc.vector.memset(wd_sc[:].bitcast(I32), 0)
         moved_sc = [sbuf([P, 2 * HALF], U8, "moved_sc%d" % h) for h in range(2)]
         for h in range(2):
             nc.vector.memset(moved_sc[h][:].bitcast(I32), 0)
-        page = [sbuf([P, T], F32, "page%d" % t) for t in range(PACK)]
-        for t in range(PACK):
-            nc.vector.memset(page[t][:], 0.0)
+        page = [sbuf([P, T], F32, "page0")]
+        nc.vector.memset(page[0][:], 0.0)
 
         lists = [sbuf([P, J // PER_COL], U16, "list%d" % s) for s in range(2)]
         tab = sbuf([P, T], I32, "tab")
         nc.sync.dma_start(lists[0][:], offs)
-        nc.sync.dma_start(lists[1][:], offs2)
-        sm_sb = sbuf([P, PACK], F32, "sm_sb")
-        nc.sync.dma_start(sm_sb[:], sm.rearrange("(p t) -> p t", t=PACK))
-        wd4 = sbuf([P, 2 * N], U8, "wd4")
-        nc.sync.dma_start(wd4[:].bitcast(I32), wd4_words[0].bitcast(I32))
         nc.sync.dma_start(tab[:], tab_words[0].rearrange("p t i -> p (t i)").bitcast(I32))
         for q in range(4):
-            nc.scalar.dma_start(
+            nc.sync.dma_start(
                 tab_sc[32 * q : 32 * q + 8, :].bitcast(I32), tab_scales[:, 4 * q : 4 * q + 4, :].bitcast(I32)
             )
+        nc.sync.dma_start(lists[1][:], offs2)
         w_raw = []
-        for s, w in enumerate((ws, wt)):
-            for a in range(2):
-                raw = sbuf([P, PACK, R], F32, "w_raw%d%d" % (s, a))
+        for a in range(2):
+            for w in (ws, wt):
+                raw = sbuf([P, PACK, R], F32, "w_raw%d" % len(w_raw))
                 nc.sync.dma_start(raw[:], w[512 * a : 512 * (a + 1), :].rearrange("(p j) r -> p j r", j=PACK))
                 w_raw.append(raw)
         wgo_sb = sbuf([P, J], F32, "wgo_sb")
         nc.sync.dma_start(wgo_sb[:], wgo)
-        r_rows = rT.rearrange("(p t) c -> p t c", t=PACK)
-        r_sb = [sbuf([P, T], F32, "r_sb%d" % t) for t in range(PACK)]
-        nc.sync.dma_start(r_sb[0][:], r_rows[:, 0, :])
+        sm_sb = sbuf([P, PACK], F32, "sm_sb")
+        nc.sync.dma_start(sm_sb[:], sm.rearrange("(p t) -> p t", t=PACK))
+        wd4 = sbuf([P, 2 * N], U8, "wd4")
+        nc.sync.dma_start(wd4[:].bitcast(I32), wd4_words[0].bitcast(I32))
         wd8 = sbuf([P, N], I32, "wd8")
         nc.sync.dma_start(wd8[:], wd8_words[0].rearrange("p n i -> p (n i)").bitcast(I32))
-        for t in range(1, PACK):
-            nc.sync.dma_start(r_sb[t][:], r_rows[:, t, :])
-        for i, scales in enumerate((wd4_scales, wd8_scales)):
+        for i, (scales, queue) in enumerate(((wd4_scales, nc.sync), (wd8_scales, nc.gpsimd))):
             for q in range(4):
-                nc.gpsimd.dma_start(
+                queue.dma_start(
                     wd_sc[32 * q : 32 * q + 4, N * i : N * (i + 1)].bitcast(I32),
                     scales[0, 4 * q : 4 * q + 4, :].bitcast(I32),
                 )
-        ident = sbuf([P, P], F32, "ident")
-        make_identity(nc, ident[:])
 
         picked_sc = [None, None]
         parted = {}
@@ -121,7 +115,8 @@ def tile_list_msg_gelu_res_resLP_kernel(
             nc.gpsimd.dma_start(moved_sc[h][0:100, :].bitcast(I32), picked[4:104, :].bitcast(I32))
             picked_sc[h] = picked
 
-        w_codes, w_scales = [], []
+        w_codes, w_scales, r_sb = [], [], []
+        r_rows = rT.rearrange("(p t) c -> p t c", t=PACK)
 
         def quantise_weight(i):
             grouped = sbuf([P, PACK * R], BF16, "w_grouped%d" % i)
@@ -134,11 +129,14 @@ def tile_list_msg_gelu_res_resLP_kernel(
             nc.vector.quantize_mx(out=codes[:].bitcast(FP8X4), scales=scales[:], in_=grouped[:])
             w_codes.append(codes)
             w_scales.append(scales)
+            rows = sbuf([P, T], F32, "r_sb%d" % i, "w_raw%d" % i)
+            nc.sync.dma_start(rows[:], r_rows[:, i, :])
+            r_sb.append(rows)
 
         acc = {}
 
         def first_layer_pass(h, i):
-            s, a = divmod(i, 2)
+            a, s = divmod(i, 2)
             plane = (picked_sc, moved_sc)[a][h]
             for t in range(PACK):
                 if i == 0:
@@ -153,16 +151,16 @@ def tile_list_msg_gelu_res_resLP_kernel(
                     stop=(i == 3),
                 )
 
-        pick_scales(0)
         first = [pick_words(s, 0) for s in range(2)]
+        pick_scales(0)
         for s in range(2):
             part_words(s, 0, first[s])
         quantise_weight(0)
         first_layer_pass(0, 0)
-        part_words(0, 1, pick_words(0, 1, "w_grouped0"))
+        pick_scales(1, "w_grouped0")
         quantise_weight(1)
         first_layer_pass(0, 1)
-        pick_scales(1, "w_grouped1")
+        part_words(0, 1, pick_words(0, 1, "w_grouped1"))
         quantise_weight(2)
         first_layer_pass(0, 2)
         late_words = pick_words(1, 1, "w_grouped2")
@@ -170,16 +168,19 @@ def tile_list_msg_gelu_res_resLP_kernel(
         first_layer_pass(0, 3)
         part_words(1, 1, late_words)
 
-        wgo_col = sbuf([P, J // P], F32, "wgo_col")
-        for g in range(2):
-            turned = bank([P, PACK, P], "wgo_turned%d" % g, PACK + g)
-            for b in range(PACK):
-                first_edge = P * (PACK * g + b)
+        late = sbuf([P, PACK * HALF + J // P], F32, "late", "w_grouped3")
+        wgo_col = late[:, PACK * HALF :]
+        for g in range(PACK):
+            turned = bank([P, 2, P], "wgo_turned%d" % g, PACK + g)
+            for b in range(2):
+                first_edge = P * (2 * g + b)
                 nc.tensor.transpose(turned[:, b, :], wgo_sb[:, first_edge : first_edge + P], ident[:])
-            nc.scalar.copy(wgo_col[:, PACK * g : PACK * (g + 1)], turned[:, :, 0])
+            nc.scalar.copy(wgo_col[:, 2 * g : 2 * (g + 1)], turned[:, :, 0])
 
-        for i in range(4):
-            first_layer_pass(1, i)
+        for t, slot in ((1, "tab"), (2, "w_grouped2"), (3, "parted00")):
+            page.append(sbuf([P, T], F32, "page%d" % t, slot))
+            for c in range(0, T, T // 4):
+                nc.gpsimd.memset(page[t][:, c : c + T // 4], 0.0)
 
         rw = {}
 
@@ -190,7 +191,7 @@ def tile_list_msg_gelu_res_resLP_kernel(
             rw[t, h] = out
 
         for t in range(PACK):
-            pick_residual(t, 0, sbuf([P, HALF], F32, "rw%d" % t)[:])
+            pick_residual(t, 0, late[:, HALF * t : HALF * (t + 1)])
 
         h_codes, h_scales, z = {}, {}, {}
 
@@ -219,7 +220,7 @@ def tile_list_msg_gelu_res_resLP_kernel(
 
         def message(q):
             z[q] = sbuf([P, PACK, QUARTER], F32, "z%d" % q)
-            y_sb = []
+            y_sb = sbuf([P, 2, PACK, P], F32, "y_sb%d" % q, "scaled%d" % ((q + 1) % 2))
             for b in range(2):
                 cols = slice(P * b, P * (b + 1))
                 y_ps = bank([P, N], "y_ps%d%d" % (q, b), b)
@@ -233,18 +234,16 @@ def tile_list_msg_gelu_res_resLP_kernel(
                         start=(i == 0),
                         stop=(i == 1),
                     )
-                weighted = sbuf([P, PACK, P], F32, "y_sb%d%d" % (q, b), "y_sb%d%d" % (q % 2, b))
                 nc.scalar.activation(
-                    weighted[:],
+                    y_sb[:, b, :, :],
                     y_ps[:].rearrange("j (p t) -> j t p", t=PACK),
                     COPY,
                     scale=wgo_col[:, 2 * q + b : 2 * q + b + 1],
                 )
-                y_sb.append(weighted)
             for b in range(2):
                 z_ps = bank([P, PACK, P], "z_ps%d%d" % (q, b), 2 + b)
                 for t in range(PACK):
-                    nc.tensor.transpose(z_ps[:, t, :], y_sb[b][:, t, :], ident[:])
+                    nc.tensor.transpose(z_ps[:, t, :], y_sb[:, b, t, :], ident[:])
                 nc.scalar.copy(z[q][:, :, P * b : P * (b + 1)], z_ps[:])
 
         def scatter(q, t):
@@ -263,6 +262,8 @@ def tile_list_msg_gelu_res_resLP_kernel(
         message(0)
         for t in range(PACK):
             scatter(0, t)
+        for i in range(4):
+            first_layer_pass(1, i)
         hidden(2)
         message(1)
         for t in range(PACK - 1):
@@ -276,8 +277,8 @@ def tile_list_msg_gelu_res_resLP_kernel(
         out_rows = out_0.rearrange("(p t) c -> p t c", t=PACK)
         split = sum(VECTOR_WIDTHS)
         rounded = [
-            sbuf([P, PACK, split], BF16, "rounded0", "w_raw00"),
-            sbuf([P, PACK, T - split], BF16, "rounded1", "w_raw01"),
+            sbuf([P, PACK, split], BF16, "rounded0", "w_raw0"),
+            sbuf([P, PACK, T - split], BF16, "rounded1", "w_raw1"),
         ]
         for t in range(PACK - 1):
             scatter(3, t)
@@ -291,17 +292,15 @@ def tile_list_msg_gelu_res_resLP_kernel(
 
         codes = sbuf([P, T], I32, "out_codes")
         scales = sbuf([P, T], U8, "out_scales")
-        free_slots = ["r_sb0", "r_sb1", "r_sb2", "r_sb3", "w_raw10", "w_raw11", "tab"]
 
-        def group(copy, source, source_first, first, width, n):
+        def group(copy, source, source_first, first, width):
             cols = slice(first - source_first, first - source_first + width)
-            copy(source[:, last, cols], page[last][:, first : first + width])
-            grouped = sbuf([P, PACK * width], BF16, "out_grouped%d" % n, free_slots[n])
+            grouped = sbuf([P, PACK * width], BF16, "out_grouped%d" % first)
             copy(
                 grouped[:].rearrange("p (c i t) -> p c t i", i=4, t=PACK),
                 source[:, :, cols].rearrange("p t (c i) -> p c t i", i=4),
             )
-            return grouped
+            return grouped, first, width
 
         def quantise_out(grouped, first, width):
             nc.vector.quantize_mx(
@@ -310,18 +309,22 @@ def tile_list_msg_gelu_res_resLP_kernel(
 
         by_scalar = []
         first_col = split
-        for n, width in enumerate(SCALAR_WIDTHS):
-            by_scalar.append((group(nc.scalar.copy, rounded[1], split, first_col, width, len(VECTOR_WIDTHS) + n), first_col, width))
+        for width in SCALAR_WIDTHS:
+            nc.scalar.copy(
+                rounded[1][:, last, first_col - split : first_col - split + width], page[last][:, first_col : first_col + width]
+            )
+            by_scalar.append(group(nc.scalar.copy, rounded[1], split, first_col, width))
+            first_col = first_col + width
+        by_vector = []
+        first_col = 0
+        for width in VECTOR_WIDTHS:
+            nc.vector.tensor_copy(rounded[0][:, last, first_col : first_col + width], page[last][:, first_col : first_col + width])
             first_col = first_col + width
         first_col = 0
-        waiting = []
-        for n, width in enumerate(VECTOR_WIDTHS):
-            grouped = group(nc.vector.tensor_copy, rounded[0], 0, first_col, width, n)
-            for item in waiting:
-                quantise_out(*item)
-            waiting = [by_scalar[n], (grouped, first_col, width)]
+        for width in VECTOR_WIDTHS:
+            by_vector.append(group(nc.vector.tensor_copy, rounded[0], 0, first_col, width))
             first_col = first_col + width
-        for item in waiting + by_scalar[len(VECTOR_WIDTHS) :]:
+        for item in by_vector + by_scalar:
             quantise_out(*item)
 
         words_out = out_1[0].rearrange("p t i -> p (t i)").bitcast(I32)

@@ -21,13 +21,18 @@ COPY = mybir.ActivationFunctionType.Copy
 
 P = 128
 PACK = 4
+K_PASS = P * PACK
+QUADS = 4
 HALF = J // 2
 QUARTER = J // 4
 PER_COL = 16
+RUN = 4
+MOVED_ROWS = 112
 
-VECTOR_WIDTHS = (512, 512, 128)
-SCALAR_WIDTHS = (256, 256, 256, 128)
-STORE_CUTS = (0, 512, 1152, 1664, 2048)
+PASS_ORDER = ((0, 1, 2, 3), (1, 0, 2, 3))
+Y_SLOTS = ("act1", "act1", "act0", "act0")
+SIDE_WIDTHS = ((512, 512, 256), (512, 256))
+STORE_WIDTH = 512
 
 
 def tile_list_msg_gelu_res_resLP_kernel(
@@ -48,6 +53,13 @@ def tile_list_msg_gelu_res_resLP_kernel(
         def entries(list_tile, first, count):
             return list_tile[:, first // PER_COL : (first + count) // PER_COL]
 
+        def interleave(copy, grouped, first_set, rows):
+            sets = rows.shape[1]
+            copy(
+                grouped[:].rearrange("p (c i t) -> p c t i", i=RUN, t=PACK)[:, :, first_set : first_set + sets, :],
+                rows.rearrange("p t (c i) -> p c t i", i=RUN),
+            )
+
         tab_sc = sbuf([P, T], U8, "tab_sc")
         nc.gpsimd.memset(tab_sc[:].bitcast(I32), 0)
         ident = sbuf([P, P], F32, "ident")
@@ -57,23 +69,25 @@ def tile_list_msg_gelu_res_resLP_kernel(
         moved_sc = [sbuf([P, 2 * HALF], U8, "moved_sc%d" % h) for h in range(2)]
         for h in range(2):
             nc.vector.memset(moved_sc[h][:].bitcast(I32), 0)
-        page = [sbuf([P, T], F32, "page0")]
-        nc.vector.memset(page[0][:], 0.0)
+        page = [sbuf([P, T], F32, "page%d" % t) for t in range(PACK - 1)]
+        for t in range(PACK - 1):
+            nc.vector.memset(page[t][:].bitcast(I32), 0)
 
         lists = [sbuf([P, J // PER_COL], U16, "list%d" % s) for s in range(2)]
         tab = sbuf([P, T], I32, "tab")
         nc.sync.dma_start(lists[0][:], offs)
         nc.sync.dma_start(tab[:], tab_words[0].rearrange("p t i -> p (t i)").bitcast(I32))
-        for q in range(4):
+        for quad in range(QUADS):
             nc.sync.dma_start(
-                tab_sc[32 * q : 32 * q + 8, :].bitcast(I32), tab_scales[:, 4 * q : 4 * q + 4, :].bitcast(I32)
+                tab_sc[32 * quad : 32 * quad + 8, :].bitcast(I32),
+                tab_scales[:, 4 * quad : 4 * quad + 4, :].bitcast(I32),
             )
         nc.sync.dma_start(lists[1][:], offs2)
         w_raw = []
         for a in range(2):
             for w in (ws, wt):
                 raw = sbuf([P, PACK, R], F32, "w_raw%d" % len(w_raw))
-                nc.sync.dma_start(raw[:], w[512 * a : 512 * (a + 1), :].rearrange("(p j) r -> p j r", j=PACK))
+                nc.sync.dma_start(raw[:], w[K_PASS * a : K_PASS * (a + 1), :].rearrange("(p j) r -> p j r", j=PACK))
                 w_raw.append(raw)
         wgo_sb = sbuf([P, J], F32, "wgo_sb")
         nc.sync.dma_start(wgo_sb[:], wgo)
@@ -83,11 +97,11 @@ def tile_list_msg_gelu_res_resLP_kernel(
         nc.sync.dma_start(wd4[:].bitcast(I32), wd4_words[0].bitcast(I32))
         wd8 = sbuf([P, N], I32, "wd8")
         nc.sync.dma_start(wd8[:], wd8_words[0].rearrange("p n i -> p (n i)").bitcast(I32))
-        for i, (scales, queue) in enumerate(((wd4_scales, nc.sync), (wd8_scales, nc.gpsimd))):
-            for q in range(4):
+        for i, (hbm_scales, queue) in enumerate(((wd4_scales, nc.sync), (wd8_scales, nc.gpsimd))):
+            for quad in range(QUADS):
                 queue.dma_start(
-                    wd_sc[32 * q : 32 * q + 4, N * i : N * (i + 1)].bitcast(I32),
-                    scales[0, 4 * q : 4 * q + 4, :].bitcast(I32),
+                    wd_sc[32 * quad : 32 * quad + 4, N * i : N * (i + 1)].bitcast(I32),
+                    hbm_scales[0, 4 * quad : 4 * quad + 4, :].bitcast(I32),
                 )
 
         picked_sc = [None, None]
@@ -98,8 +112,8 @@ def tile_list_msg_gelu_res_resLP_kernel(
             nc.vector.tensor_copy(words[:], tab[:].bitcast(U32).indirect(entries(lists[s], HALF * h, HALF)))
             return words
 
-        def part_words(s, h, words):
-            both = sbuf([P, 2 * 2 * HALF], U8, "parted%d%d" % (s, h))
+        def part_words(s, h, words, slot=None):
+            both = sbuf([P, 2 * 2 * HALF], U8, "parted%d%d" % (s, h), slot)
             nc.vector.tensor_copy(
                 both[:].bitcast(U16).rearrange("p (d j) -> p d j", d=2),
                 words[:].bitcast(U16).rearrange("p (j d) -> p d j", d=2),
@@ -112,7 +126,7 @@ def tile_list_msg_gelu_res_resLP_kernel(
                 nc.vector.tensor_copy(
                     picked[:, HALF * s : HALF * (s + 1)], tab_sc[:].indirect(entries(lists[s], HALF * h, HALF))
                 )
-            nc.gpsimd.dma_start(moved_sc[h][0:100, :].bitcast(I32), picked[4:104, :].bitcast(I32))
+            nc.sync.dma_start(moved_sc[h][0:MOVED_ROWS, :].bitcast(I32), picked[4 : 4 + MOVED_ROWS, :].bitcast(I32))
             picked_sc[h] = picked
 
         w_codes, w_scales, r_sb = [], [], []
@@ -135,11 +149,12 @@ def tile_list_msg_gelu_res_resLP_kernel(
 
         acc = {}
 
-        def first_layer_pass(h, i):
+        def first_layer_pass(h, step):
+            i = PASS_ORDER[h][step]
             a, s = divmod(i, 2)
             plane = (picked_sc, moved_sc)[a][h]
             for t in range(PACK):
-                if i == 0:
+                if step == 0:
                     acc[h, t] = bank([P, HALF], "acc%d%d" % (h, t), PACK * h + t)
                 nc.tensor.matmul_mx(
                     out=acc[h, t][:],
@@ -147,14 +162,14 @@ def tile_list_msg_gelu_res_resLP_kernel(
                     lhsT_scale=w_scales[i][:, P * t : P * (t + 1)],
                     rhs=parted[s, h][:, 2 * HALF * a : 2 * HALF * (a + 1)].bitcast(FP4X4),
                     rhs_scale=plane[:, HALF * s : HALF * (s + 1)],
-                    start=(i == 0),
-                    stop=(i == 3),
+                    start=(step == 0),
+                    stop=(step == 3),
                 )
 
-        first = [pick_words(s, 0) for s in range(2)]
+        first_words = [pick_words(s, 0) for s in range(2)]
         pick_scales(0)
         for s in range(2):
-            part_words(s, 0, first[s])
+            part_words(s, 0, first_words[s])
         quantise_weight(0)
         first_layer_pass(0, 0)
         pick_scales(1, "w_grouped0")
@@ -166,36 +181,30 @@ def tile_list_msg_gelu_res_resLP_kernel(
         late_words = pick_words(1, 1, "w_grouped2")
         quantise_weight(3)
         first_layer_pass(0, 3)
-        part_words(1, 1, late_words)
+        part_words(1, 1, late_words, "parted10")
 
-        late = sbuf([P, PACK * HALF + J // P], F32, "late", "w_grouped3")
-        wgo_col = late[:, PACK * HALF :]
-        for g in range(PACK):
-            turned = bank([P, 2, P], "wgo_turned%d" % g, PACK + g)
-            for b in range(2):
-                first_edge = P * (2 * g + b)
+        wgo_col = sbuf([P, J // P], F32, "wgo_col")
+        for g in range(2):
+            turned = bank([P, PACK, P], "wgo_turned%d" % g, PACK + g)
+            for b in range(PACK):
+                first_edge = P * (PACK * g + b)
                 nc.tensor.transpose(turned[:, b, :], wgo_sb[:, first_edge : first_edge + P], ident[:])
-            nc.scalar.copy(wgo_col[:, 2 * g : 2 * (g + 1)], turned[:, :, 0])
+            nc.scalar.copy(wgo_col[:, PACK * g : PACK * (g + 1)], turned[:, :, 0])
 
-        for t, slot in ((1, "tab"), (2, "w_grouped2"), (3, "parted00")):
-            page.append(sbuf([P, T], F32, "page%d" % t, slot))
-            for c in range(0, T, T // 4):
-                nc.gpsimd.memset(page[t][:, c : c + T // 4], 0.0)
+        page.append(sbuf([P, T], F32, "page3", "parted00"))
+        for c in range(0, T, T // 4):
+            nc.gpsimd.memset(page[3][:, c : c + T // 4], 0.0)
 
-        rw = {}
+        rw = []
 
-        def pick_residual(t, h, out):
-            nc.vector.tensor_tensor(
-                out, r_sb[t][:].indirect(entries(lists[1], HALF * h, HALF)), wgo_sb[:, HALF * h : HALF * (h + 1)], MULT
-            )
-            rw[t, h] = out
-
-        for t in range(PACK):
-            pick_residual(t, 0, late[:, HALF * t : HALF * (t + 1)])
+        def pick_residual(t, slot=None):
+            picked = sbuf([P, J], F32, "rw%d" % t, slot)
+            nc.vector.tensor_tensor(picked[:], r_sb[t][:].indirect(lists[1][:]), wgo_sb[:], MULT)
+            rw.append(picked)
 
         h_codes, h_scales, z = {}, {}, {}
 
-        def hidden(q):
+        def hidden(q, slot=None):
             h, c = divmod(q, 2)
             cols = slice(QUARTER * c, QUARTER * (c + 1))
             act = sbuf([P, PACK, QUARTER], F32, "act%d" % q, "act%d" % (q % 2))
@@ -204,23 +213,15 @@ def tile_list_msg_gelu_res_resLP_kernel(
                 nc.scalar.activation(act[:, t, :], acc[h, t][:, cols], GELU)
             for t in range(PACK):
                 nc.scalar.activation(scaled[:, t, :], act[:, t, :], COPY, scale=sm_sb[:, t : t + 1])
-            grouped = sbuf([P, PACK * QUARTER], BF16, "h_grouped%d" % q)
-            nc.scalar.copy(
-                grouped[:].rearrange("p (c i t) -> p c t i", i=4, t=PACK),
-                scaled[:].rearrange("p t (c i) -> p c t i", i=4),
-            )
+            grouped = sbuf([P, PACK * QUARTER], BF16, "h_grouped%d" % q, slot)
+            interleave(nc.vector.tensor_copy, grouped, 0, scaled[:])
             h_codes[q] = sbuf([P, QUARTER], U32, "h_codes%d" % q)
             h_scales[q] = sbuf([P, QUARTER], U8, "h_scales%d" % q)
             nc.vector.quantize_mx(out=h_codes[q][:].bitcast(FP8X4), scales=h_scales[q][:], in_=grouped[:])
 
-        def late_residuals(q):
-            pair = sbuf([P, 2, HALF], F32, "rw_late%d" % q, "h_grouped%d" % q)
-            for i in range(2):
-                pick_residual(2 * q + i, 1, pair[:, i, :])
-
         def message(q):
             z[q] = sbuf([P, PACK, QUARTER], F32, "z%d" % q)
-            y_sb = sbuf([P, 2, PACK, P], F32, "y_sb%d" % q, "scaled%d" % ((q + 1) % 2))
+            y_sb = sbuf([P, 2, PACK, P], F32, "y_sb%d" % q, Y_SLOTS[q])
             for b in range(2):
                 cols = slice(P * b, P * (b + 1))
                 y_ps = bank([P, N], "y_ps%d%d" % (q, b), b)
@@ -247,88 +248,76 @@ def tile_list_msg_gelu_res_resLP_kernel(
                 nc.scalar.copy(z[q][:, :, P * b : P * (b + 1)], z_ps[:])
 
         def scatter(q, t):
-            h, c = divmod(q, 2)
             nc.vector.tensor_tensor(
                 page[t][:].indirect(entries(lists[1], QUARTER * q, QUARTER)),
                 z[q][:, t, :],
-                rw[t, h][:, QUARTER * c : QUARTER * (c + 1)],
+                rw[t][:, QUARTER * q : QUARTER * (q + 1)],
                 ADD,
             )
 
-        hidden(0)
-        late_residuals(0)
-        hidden(1)
-        late_residuals(1)
+        pick_residual(0, "w_grouped3")
+        pick_residual(1)
+        hidden(0, "w_raw1")
+        pick_residual(2, "w_raw1")
+        hidden(1, "w_raw2")
         message(0)
-        for t in range(PACK):
+        for t in range(3):
             scatter(0, t)
-        for i in range(4):
-            first_layer_pass(1, i)
+        for step in range(4):
+            first_layer_pass(1, step)
         hidden(2)
-        message(1)
-        for t in range(PACK - 1):
-            scatter(1, t)
+        pick_residual(3, "h_grouped2")
         hidden(3)
-        message(2)
-        for t in range(PACK - 1):
-            scatter(2, t)
-        message(3)
+        for q in range(1, 4):
+            message(q)
+            for t in range(2):
+                scatter(q, t)
 
         out_rows = out_0.rearrange("(p t) c -> p t c", t=PACK)
-        split = sum(VECTOR_WIDTHS)
-        rounded = [
-            sbuf([P, PACK, split], BF16, "rounded0", "w_raw0"),
-            sbuf([P, PACK, T - split], BF16, "rounded1", "w_raw1"),
-        ]
-        for t in range(PACK - 1):
-            scatter(3, t)
+        side_slots = ("w_raw0", "w_raw3")
+        side_cols = (slice(0, sum(SIDE_WIDTHS[0])), slice(sum(SIDE_WIDTHS[0]), T))
+        pieces = []
+        for side, widths in enumerate(SIDE_WIDTHS):
+            for n, width in enumerate(widths):
+                start = sum(widths[:n])
+                pieces.append((side, start, width, sbuf([P, PACK * width], BF16, "out_grouped%d%d" % (side, n))))
+
+        low = [sbuf([P, 2, sum(SIDE_WIDTHS[side])], BF16, "rounded_low%d" % side, side_slots[side]) for side in range(2)]
+        for t in range(2):
             nc.sync.dma_start(out_rows[:, t, :], page[t][:])
-            nc.scalar.copy(rounded[0][:, t, :], page[t][:, 0:split])
-            nc.scalar.copy(rounded[1][:, t, :], page[t][:, split:T])
-        last = PACK - 1
-        for q in (3, 1, 2):
-            scatter(q, last)
-        nc.sync.dma_start(out_rows[:, last, :], page[last][:])
+            for side in range(2):
+                nc.scalar.copy(low[side][:, t, :], page[t][:, side_cols[side]])
+        for side, start, width, grouped in pieces:
+            interleave(nc.scalar.copy, grouped, 0, low[side][:, :, start : start + width])
 
-        codes = sbuf([P, T], I32, "out_codes")
-        scales = sbuf([P, T], U8, "out_scales")
+        for q2, q3 in ((3, 3), (1, 0), (2, 1)):
+            scatter(q2, 2)
+            scatter(q3, 3)
+        scatter(2, 3)
+        high = [sbuf([P, 2, sum(SIDE_WIDTHS[side])], BF16, "rounded_high%d" % side, side_slots[side]) for side in range(2)]
+        nc.sync.dma_start(out_rows[:, 2, :], page[2][:])
+        for side in range(2):
+            nc.scalar.copy(high[side][:, 0, :], page[2][:, side_cols[side]])
+        nc.sync.dma_start(out_rows[:, 3, :], page[3][:])
 
-        def group(copy, source, source_first, first, width):
-            cols = slice(first - source_first, first - source_first + width)
-            grouped = sbuf([P, PACK * width], BF16, "out_grouped%d" % first)
-            copy(
-                grouped[:].rearrange("p (c i t) -> p c t i", i=4, t=PACK),
-                source[:, :, cols].rearrange("p t (c i) -> p c t i", i=4),
-            )
-            return grouped, first, width
+        for side, copy in enumerate((nc.vector.tensor_copy, nc.scalar.copy)):
+            mine = [piece[1:] for piece in pieces if piece[0] == side]
+            for start, width, grouped in mine:
+                first_col = side_cols[side].start + start
+                copy(high[side][:, 1, start : start + width], page[3][:, first_col : first_col + width])
+            for start, width, grouped in mine:
+                interleave(copy, grouped, 2, high[side][:, :, start : start + width])
 
-        def quantise_out(grouped, first, width):
-            nc.vector.quantize_mx(
-                out=codes[:, first : first + width].bitcast(FP8X4), scales=scales[:, first : first + width], in_=grouped[:]
-            )
-
-        by_scalar = []
-        first_col = split
-        for width in SCALAR_WIDTHS:
-            nc.scalar.copy(
-                rounded[1][:, last, first_col - split : first_col - split + width], page[last][:, first_col : first_col + width]
-            )
-            by_scalar.append(group(nc.scalar.copy, rounded[1], split, first_col, width))
-            first_col = first_col + width
-        by_vector = []
-        first_col = 0
-        for width in VECTOR_WIDTHS:
-            nc.vector.tensor_copy(rounded[0][:, last, first_col : first_col + width], page[last][:, first_col : first_col + width])
-            first_col = first_col + width
-        first_col = 0
-        for width in VECTOR_WIDTHS:
-            by_vector.append(group(nc.vector.tensor_copy, rounded[0], 0, first_col, width))
-            first_col = first_col + width
-        for item in by_vector + by_scalar:
-            quantise_out(*item)
+        out_codes = sbuf([P, T], I32, "out_codes")
+        out_scales = sbuf([P, T], U8, "out_scales")
+        for side, start, width, grouped in pieces:
+            cols = slice(side_cols[side].start + start, side_cols[side].start + start + width)
+            nc.vector.quantize_mx(out=out_codes[:, cols].bitcast(FP8X4), scales=out_scales[:, cols], in_=grouped[:])
 
         words_out = out_1[0].rearrange("p t i -> p (t i)").bitcast(I32)
-        for lo, hi in zip(STORE_CUTS, STORE_CUTS[1:]):
-            nc.sync.dma_start(words_out[:, lo:hi], codes[:, lo:hi])
-        for q in range(4):
-            nc.scalar.dma_start(out_2[0, 4 * q : 4 * q + 4, :].bitcast(I32), scales[32 * q : 32 * q + 4, :].bitcast(I32))
+        for c in range(0, T, STORE_WIDTH):
+            nc.sync.dma_start(words_out[:, c : c + STORE_WIDTH], out_codes[:, c : c + STORE_WIDTH])
+        for quad in range(QUADS):
+            nc.scalar.dma_start(
+                out_2[0, 4 * quad : 4 * quad + 4, :].bitcast(I32), out_scales[32 * quad : 32 * quad + 4, :].bitcast(I32)
+            )

@@ -28,11 +28,7 @@ QUARTER = J // 4
 PER_COL = 16
 RUN = 4
 MOVED_ROWS = 112
-
-PASS_ORDER = ((0, 1, 2, 3), (1, 0, 2, 3))
-Y_SLOTS = ("act1", "act1", "act0", "act0")
-SIDE_WIDTHS = ((512, 512, 256), (512, 256))
-STORE_WIDTH = 512
+OUT_PIECES = ((512, 0), (512, 0), (512, 1), (256, 1), (256, 1))
 
 
 def tile_list_msg_gelu_res_resLP_kernel(
@@ -53,58 +49,83 @@ def tile_list_msg_gelu_res_resLP_kernel(
         def entries(list_tile, first, count):
             return list_tile[:, first // PER_COL : (first + count) // PER_COL]
 
-        def interleave(copy, grouped, first_set, rows):
-            sets = rows.shape[1]
+        def weave_words(copy, dtype, grouped, pairs):
             copy(
-                grouped[:].rearrange("p (c i t) -> p c t i", i=RUN, t=PACK)[:, :, first_set : first_set + sets, :],
-                rows.rearrange("p t (c i) -> p c t i", i=RUN),
+                grouped[:].bitcast(dtype).rearrange("p (c u) -> p c u", u=2),
+                pairs[:].bitcast(dtype).rearrange("p (u c) -> p c u", u=2),
             )
+
+        def pair_slot(pairs, t):
+            return pairs[:].rearrange("p (u c e) -> p u c e", u=2, e=2)[:, t // 2, :, t % 2]
 
         tab_sc = sbuf([P, T], U8, "tab_sc")
         nc.gpsimd.memset(tab_sc[:].bitcast(I32), 0)
+        wgo_rows = sbuf([P, P], F32, "wgo_rows")
+        nc.gpsimd.memset(wgo_rows[:], 0.0)
         ident = sbuf([P, P], F32, "ident")
         make_identity(nc, ident[:])
         wd_sc = sbuf([P, 2 * N], U8, "wd_sc")
-        nc.vector.memset(wd_sc[:].bitcast(I32), 0)
-        moved_sc = [sbuf([P, 2 * HALF], U8, "moved_sc%d" % h) for h in range(2)]
-        for h in range(2):
-            nc.vector.memset(moved_sc[h][:].bitcast(I32), 0)
-        page = [sbuf([P, T], F32, "page%d" % t) for t in range(PACK - 1)]
-        for t in range(PACK - 1):
+        nc.gpsimd.memset(wd_sc[:].bitcast(I32), 0)
+        moved_sc = sbuf([P, 2 * J], U8, "moved_sc")
+        nc.gpsimd.memset(moved_sc[:].bitcast(I32), 0)
+        page = [sbuf([P, T], F32, "page%d" % t) for t in range(PACK)]
+        for t in range(2):
             nc.vector.memset(page[t][:].bitcast(I32), 0)
+        for t in range(2, PACK):
+            for c in range(0, T, T // 4):
+                nc.gpsimd.memset(page[t][:, c : c + T // 4], 0.0)
 
         lists = [sbuf([P, J // PER_COL], U16, "list%d" % s) for s in range(2)]
         tab = sbuf([P, T], I32, "tab")
+        w_raw = [sbuf([P, PACK, R], F32, "w_raw%d" % i) for i in range(4)]
+
+        def load_weight(i):
+            a, s = divmod(i, 2)
+            rows = (ws, wt)[s][K_PASS * a : K_PASS * (a + 1), :]
+            nc.sync.dma_start(w_raw[i][:], rows.rearrange("(p j) r -> p j r", j=PACK))
+
         nc.sync.dma_start(lists[0][:], offs)
-        nc.sync.dma_start(tab[:], tab_words[0].rearrange("p t i -> p (t i)").bitcast(I32))
         for quad in range(QUADS):
             nc.sync.dma_start(
                 tab_sc[32 * quad : 32 * quad + 8, :].bitcast(I32),
                 tab_scales[:, 4 * quad : 4 * quad + 4, :].bitcast(I32),
             )
+        load_weight(0)
         nc.sync.dma_start(lists[1][:], offs2)
-        w_raw = []
-        for a in range(2):
-            for w in (ws, wt):
-                raw = sbuf([P, PACK, R], F32, "w_raw%d" % len(w_raw))
-                nc.sync.dma_start(raw[:], w[K_PASS * a : K_PASS * (a + 1), :].rearrange("(p j) r -> p j r", j=PACK))
-                w_raw.append(raw)
-        wgo_sb = sbuf([P, J], F32, "wgo_sb")
-        nc.sync.dma_start(wgo_sb[:], wgo)
-        sm_sb = sbuf([P, PACK], F32, "sm_sb")
-        nc.sync.dma_start(sm_sb[:], sm.rearrange("(p t) -> p t", t=PACK))
+        nc.sync.dma_start(tab[:], tab_words[0].rearrange("p t i -> p (t i)").bitcast(I32))
+        nc.sync.dma_start(wgo_rows[0 : J // P, :], wgo[0].rearrange("(b c) -> b c", c=P))
+        for i in range(1, 4):
+            load_weight(i)
         wd4 = sbuf([P, 2 * N], U8, "wd4")
         nc.sync.dma_start(wd4[:].bitcast(I32), wd4_words[0].bitcast(I32))
         wd8 = sbuf([P, N], I32, "wd8")
         nc.sync.dma_start(wd8[:], wd8_words[0].rearrange("p n i -> p (n i)").bitcast(I32))
-        for i, (hbm_scales, queue) in enumerate(((wd4_scales, nc.sync), (wd8_scales, nc.gpsimd))):
+        sm_sb = sbuf([P, PACK], F32, "sm_sb")
+        nc.gpsimd.dma_start(sm_sb[:], sm.rearrange("(p t) -> p t", t=PACK))
+        for i, hbm_scales in enumerate((wd4_scales, wd8_scales)):
             for quad in range(QUADS):
-                queue.dma_start(
+                nc.gpsimd.dma_start(
                     wd_sc[32 * quad : 32 * quad + 4, N * i : N * (i + 1)].bitcast(I32),
                     hbm_scales[0, 4 * quad : 4 * quad + 4, :].bitcast(I32),
                 )
 
-        picked_sc = [None, None]
+        wgo_col = sbuf([P, J // P], F32, "wgo_col")
+        turned = bank([P, P], "wgo_turned", 4)
+        nc.tensor.transpose(turned[:], wgo_rows[:], ident[:])
+        nc.scalar.copy(wgo_col[:], turned[:, 0 : J // P])
+        wgo_sb = sbuf([P, J], F32, "wgo_sb")
+        for g in range(2):
+            spread = bank([P, PACK, P], "wgo_spread%d" % g, 5 + g)
+            for b in range(PACK):
+                col = PACK * g + b
+                nc.tensor.transpose(spread[:, b, :], wgo_col[:, col : col + 1].to_broadcast([P, P]), ident[:])
+            nc.scalar.copy(wgo_sb[:, HALF * g : HALF * (g + 1)], spread[:].rearrange("p b c -> p (b c)"))
+
+        picked_sc = sbuf([P, 2 * J], U8, "picked_sc")
+        for s in range(2):
+            nc.vector.tensor_copy(picked_sc[:, J * s : J * (s + 1)], tab_sc[:].indirect(lists[s][:]))
+        nc.sync.dma_start(moved_sc[0:MOVED_ROWS, :].bitcast(I32), picked_sc[4 : 4 + MOVED_ROWS, :].bitcast(I32))
+
         parted = {}
 
         def pick_words(s, h, slot=None):
@@ -112,22 +133,13 @@ def tile_list_msg_gelu_res_resLP_kernel(
             nc.vector.tensor_copy(words[:], tab[:].bitcast(U32).indirect(entries(lists[s], HALF * h, HALF)))
             return words
 
-        def part_words(s, h, words, slot=None):
-            both = sbuf([P, 2 * 2 * HALF], U8, "parted%d%d" % (s, h), slot)
+        def part_words(s, h, words):
+            both = sbuf([P, 2 * 2 * HALF], U8, "parted%d%d" % (s, h))
             nc.vector.tensor_copy(
                 both[:].bitcast(U16).rearrange("p (d j) -> p d j", d=2),
                 words[:].bitcast(U16).rearrange("p (j d) -> p d j", d=2),
             )
             parted[s, h] = both
-
-        def pick_scales(h, slot=None):
-            picked = sbuf([P, 2 * HALF], U8, "picked_sc%d" % h, slot)
-            for s in range(2):
-                nc.vector.tensor_copy(
-                    picked[:, HALF * s : HALF * (s + 1)], tab_sc[:].indirect(entries(lists[s], HALF * h, HALF))
-                )
-            nc.sync.dma_start(moved_sc[h][0:MOVED_ROWS, :].bitcast(I32), picked[4 : 4 + MOVED_ROWS, :].bitcast(I32))
-            picked_sc[h] = picked
 
         w_codes, w_scales, r_sb = [], [], []
         r_rows = rT.rearrange("(p t) c -> p t c", t=PACK)
@@ -149,51 +161,32 @@ def tile_list_msg_gelu_res_resLP_kernel(
 
         acc = {}
 
-        def first_layer_pass(h, step):
-            i = PASS_ORDER[h][step]
+        def first_layer(h, t, i):
             a, s = divmod(i, 2)
-            plane = (picked_sc, moved_sc)[a][h]
-            for t in range(PACK):
-                if step == 0:
-                    acc[h, t] = bank([P, HALF], "acc%d%d" % (h, t), PACK * h + t)
-                nc.tensor.matmul_mx(
-                    out=acc[h, t][:],
-                    lhsT=w_codes[i][:, P * t : P * (t + 1)].bitcast(FP8X4),
-                    lhsT_scale=w_scales[i][:, P * t : P * (t + 1)],
-                    rhs=parted[s, h][:, 2 * HALF * a : 2 * HALF * (a + 1)].bitcast(FP4X4),
-                    rhs_scale=plane[:, HALF * s : HALF * (s + 1)],
-                    start=(step == 0),
-                    stop=(step == 3),
-                )
+            if i == 0:
+                acc[h, t] = bank([P, HALF], "acc%d%d" % (h, t), t)
+            first = J * s + HALF * h
+            nc.tensor.matmul_mx(
+                out=acc[h, t][:],
+                lhsT=w_codes[i][:, P * t : P * (t + 1)].bitcast(FP8X4),
+                lhsT_scale=w_scales[i][:, P * t : P * (t + 1)],
+                rhs=parted[s, h][:, 2 * HALF * a : 2 * HALF * (a + 1)].bitcast(FP4X4),
+                rhs_scale=(picked_sc, moved_sc)[a][:, first : first + HALF],
+                start=(i == 0),
+                stop=(i == 3),
+            )
 
         first_words = [pick_words(s, 0) for s in range(2)]
-        pick_scales(0)
         for s in range(2):
             part_words(s, 0, first_words[s])
-        quantise_weight(0)
-        first_layer_pass(0, 0)
-        pick_scales(1, "w_grouped0")
-        quantise_weight(1)
-        first_layer_pass(0, 1)
-        part_words(0, 1, pick_words(0, 1, "w_grouped1"))
-        quantise_weight(2)
-        first_layer_pass(0, 2)
-        late_words = pick_words(1, 1, "w_grouped2")
-        quantise_weight(3)
-        first_layer_pass(0, 3)
-        part_words(1, 1, late_words, "parted10")
-
-        wgo_col = sbuf([P, J // P], F32, "wgo_col")
-        for g in range(2):
-            turned = bank([P, PACK, P], "wgo_turned%d" % g, PACK + g)
-            for b in range(PACK):
-                first_edge = P * (PACK * g + b)
-                nc.tensor.transpose(turned[:, b, :], wgo_sb[:, first_edge : first_edge + P], ident[:])
-            nc.scalar.copy(wgo_col[:, PACK * g : PACK * (g + 1)], turned[:, :, 0])
-
-        page.append(sbuf([P, T], F32, "page3", "parted00"))
-        for c in range(0, T, T // 4):
-            nc.gpsimd.memset(page[3][:, c : c + T // 4], 0.0)
+        for i in range(4):
+            quantise_weight(i)
+            for t in range(PACK):
+                first_layer(0, t, i)
+            if i == 0:
+                part_words(0, 1, pick_words(0, 1))
+            if i == 1:
+                part_words(1, 1, pick_words(1, 1, "w_grouped1"))
 
         rw = []
 
@@ -202,29 +195,31 @@ def tile_list_msg_gelu_res_resLP_kernel(
             nc.vector.tensor_tensor(picked[:], r_sb[t][:].indirect(lists[1][:]), wgo_sb[:], MULT)
             rw.append(picked)
 
-        h_codes, h_scales, z = {}, {}, {}
+        act = [sbuf([P, PACK, HALF], F32, "act%d" % h) for h in range(2)]
+        h_codes, h_scales, y_sb, z_low = {}, {}, {}, {}
+        z2 = [sbuf([P, HALF], F32, "z2_%d" % h) for h in range(2)]
+        z3 = sbuf([P, J], F32, "z3")
 
-        def hidden(q, slot=None):
+        def gelu(h, t):
+            nc.scalar.activation(act[h][:, t, :], acc[h, t][:], GELU)
+
+        def hidden(q):
             h, c = divmod(q, 2)
-            cols = slice(QUARTER * c, QUARTER * (c + 1))
-            act = sbuf([P, PACK, QUARTER], F32, "act%d" % q, "act%d" % (q % 2))
-            scaled = sbuf([P, PACK, QUARTER], BF16, "scaled%d" % q, "scaled%d" % (q % 2))
+            pairs = sbuf([P, PACK * QUARTER], BF16, "h_pairs%d" % q)
             for t in range(PACK):
-                nc.scalar.activation(act[:, t, :], acc[h, t][:, cols], GELU)
-            for t in range(PACK):
-                nc.scalar.activation(scaled[:, t, :], act[:, t, :], COPY, scale=sm_sb[:, t : t + 1])
-            grouped = sbuf([P, PACK * QUARTER], BF16, "h_grouped%d" % q, slot)
-            interleave(nc.vector.tensor_copy, grouped, 0, scaled[:])
+                nc.scalar.activation(
+                    pair_slot(pairs, t), act[h][:, t, QUARTER * c : QUARTER * (c + 1)], COPY, scale=sm_sb[:, t : t + 1]
+                )
+            grouped = sbuf([P, PACK * QUARTER], BF16, "h_grouped%d" % q)
+            weave_words(nc.scalar.copy, U32, grouped, pairs)
             h_codes[q] = sbuf([P, QUARTER], U32, "h_codes%d" % q)
             h_scales[q] = sbuf([P, QUARTER], U8, "h_scales%d" % q)
             nc.vector.quantize_mx(out=h_codes[q][:].bitcast(FP8X4), scales=h_scales[q][:], in_=grouped[:])
 
-        def message(q):
-            z[q] = sbuf([P, PACK, QUARTER], F32, "z%d" % q)
-            y_sb = sbuf([P, 2, PACK, P], F32, "y_sb%d" % q, Y_SLOTS[q])
+        def second_layer(q):
             for b in range(2):
                 cols = slice(P * b, P * (b + 1))
-                y_ps = bank([P, N], "y_ps%d%d" % (q, b), b)
+                y_ps = bank([P, N], "y_ps%d%d" % (q, b), 4 + b)
                 for i, (words, fmt) in enumerate(((wd4, FP4X4), (wd8, FP8X4))):
                     nc.tensor.matmul_mx(
                         out=y_ps[:],
@@ -235,88 +230,97 @@ def tile_list_msg_gelu_res_resLP_kernel(
                         start=(i == 0),
                         stop=(i == 1),
                     )
+                block = 2 * q + b
+                y_sb[block] = sbuf([P, PACK, P], F32, "y_sb%d" % block)
                 nc.scalar.activation(
-                    y_sb[:, b, :, :],
+                    y_sb[block][:],
                     y_ps[:].rearrange("j (p t) -> j t p", t=PACK),
                     COPY,
-                    scale=wgo_col[:, 2 * q + b : 2 * q + b + 1],
+                    scale=wgo_col[:, block : block + 1],
                 )
-            for b in range(2):
-                z_ps = bank([P, PACK, P], "z_ps%d%d" % (q, b), 2 + b)
-                for t in range(PACK):
-                    nc.tensor.transpose(z_ps[:, t, :], y_sb[:, b, t, :], ident[:])
-                nc.scalar.copy(z[q][:, :, P * b : P * (b + 1)], z_ps[:])
 
-        def scatter(q, t):
+        def turn_low(q):
+            z_ps = bank([P, 2, QUARTER], "z_low_ps%d" % q, 6)
+            for b in range(2):
+                for t in range(2):
+                    nc.tensor.transpose(z_ps[:, t, P * b : P * (b + 1)], y_sb[2 * q + b][:, t, :], ident[:])
+            z_low[q] = sbuf([P, 2, QUARTER], F32, "z_low%d" % q)
+            nc.scalar.copy(z_low[q][:], z_ps[:])
+            for t in range(2):
+                scatter(t, QUARTER * q, QUARTER, z_low[q][:, t, :])
+
+        def turn_high(h, t, index, dest):
+            z_ps = bank([P, HALF], "z_high_ps%d%d" % (h, t), index)
+            for b in range(PACK):
+                nc.tensor.transpose(z_ps[:, P * b : P * (b + 1)], y_sb[PACK * h + b][:, t, :], ident[:])
+            nc.scalar.copy(dest, z_ps[:])
+
+        def scatter(t, first, count, z):
             nc.vector.tensor_tensor(
-                page[t][:].indirect(entries(lists[1], QUARTER * q, QUARTER)),
-                z[q][:, t, :],
-                rw[t][:, QUARTER * q : QUARTER * (q + 1)],
-                ADD,
+                page[t][:].indirect(entries(lists[1], first, count)), z, rw[t][:, first : first + count], ADD
             )
 
-        pick_residual(0, "w_grouped3")
-        pick_residual(1)
-        hidden(0, "w_raw1")
-        pick_residual(2, "w_raw1")
-        hidden(1, "w_raw2")
-        message(0)
         for t in range(3):
-            scatter(0, t)
-        for step in range(4):
-            first_layer_pass(1, step)
+            pick_residual(t)
+        for t in range(PACK):
+            gelu(0, t)
+        hidden(0)
+        pick_residual(3, "h_pairs0")
+        hidden(1)
+        for t in range(PACK):
+            for i in range(4):
+                first_layer(1, t, i)
+        second_layer(0)
+        gelu(1, 0)
+        turn_low(0)
+        gelu(1, 1)
+        second_layer(1)
+        gelu(1, 2)
+        turn_low(1)
+        gelu(1, 3)
         hidden(2)
-        pick_residual(3, "h_grouped2")
+        turn_high(0, 2, 7, z2[0][:])
+        scatter(2, 0, HALF, z2[0][:])
         hidden(3)
-        for q in range(1, 4):
-            message(q)
-            for t in range(2):
-                scatter(q, t)
+        second_layer(2)
+        turn_high(0, 3, 0, z3[:, 0:HALF])
+        turn_low(2)
+        second_layer(3)
+        turn_low(3)
+        turn_high(1, 2, 1, z2[1][:])
+        scatter(2, HALF, HALF, z2[1][:])
+        turn_high(1, 3, 2, z3[:, HALF:J])
+        scatter(3, 0, J, z3[:])
 
         out_rows = out_0.rearrange("(p t) c -> p t c", t=PACK)
-        side_slots = ("w_raw0", "w_raw3")
-        side_cols = (slice(0, sum(SIDE_WIDTHS[0])), slice(sum(SIDE_WIDTHS[0]), T))
         pieces = []
-        for side, widths in enumerate(SIDE_WIDTHS):
-            for n, width in enumerate(widths):
-                start = sum(widths[:n])
-                pieces.append((side, start, width, sbuf([P, PACK * width], BF16, "out_grouped%d%d" % (side, n))))
-
-        low = [sbuf([P, 2, sum(SIDE_WIDTHS[side])], BF16, "rounded_low%d" % side, side_slots[side]) for side in range(2)]
-        for t in range(2):
+        pair_slots = ("w_raw0", "w_raw1", "w_raw2", "w_raw3", "tab")
+        group_slots = ("w_grouped0", "w_grouped1", "w_grouped2", "w_grouped3", "words00")
+        for n, (width, side) in enumerate(OUT_PIECES):
+            start = sum(w for w, s in OUT_PIECES[:n])
+            pairs = sbuf([P, PACK * width], BF16, "out_pairs%d" % n, pair_slots[n])
+            grouped = sbuf([P, PACK * width], BF16, "out_grouped%d" % n, group_slots[n])
+            pieces.append((slice(start, start + width), side, pairs, grouped))
+        for t in range(PACK):
             nc.sync.dma_start(out_rows[:, t, :], page[t][:])
-            for side in range(2):
-                nc.scalar.copy(low[side][:, t, :], page[t][:, side_cols[side]])
-        for side, start, width, grouped in pieces:
-            interleave(nc.scalar.copy, grouped, 0, low[side][:, :, start : start + width])
-
-        for q2, q3 in ((3, 3), (1, 0), (2, 1)):
-            scatter(q2, 2)
-            scatter(q3, 3)
-        scatter(2, 3)
-        high = [sbuf([P, 2, sum(SIDE_WIDTHS[side])], BF16, "rounded_high%d" % side, side_slots[side]) for side in range(2)]
-        nc.sync.dma_start(out_rows[:, 2, :], page[2][:])
-        for side in range(2):
-            nc.scalar.copy(high[side][:, 0, :], page[2][:, side_cols[side]])
-        nc.sync.dma_start(out_rows[:, 3, :], page[3][:])
-
-        for side, copy in enumerate((nc.vector.tensor_copy, nc.scalar.copy)):
-            mine = [piece[1:] for piece in pieces if piece[0] == side]
-            for start, width, grouped in mine:
-                first_col = side_cols[side].start + start
-                copy(high[side][:, 1, start : start + width], page[3][:, first_col : first_col + width])
-            for start, width, grouped in mine:
-                interleave(copy, grouped, 2, high[side][:, :, start : start + width])
-
+            for cols, side, pairs, grouped in pieces:
+                if side == 0 and t == 2:
+                    width = cols.stop - cols.start
+                    nc.scalar.copy(
+                        pairs[:].rearrange("p (u c e) -> p u c e", u=2, e=2)[:, 1, :, :],
+                        page[t][:, cols].unsqueeze(2).to_broadcast([P, width, 2]),
+                    )
+                else:
+                    copy = nc.vector.tensor_copy if (t == 3 and side == 0) else nc.scalar.copy
+                    copy(pair_slot(pairs, t), page[t][:, cols])
         out_codes = sbuf([P, T], I32, "out_codes")
         out_scales = sbuf([P, T], U8, "out_scales")
-        for side, start, width, grouped in pieces:
-            cols = slice(side_cols[side].start + start, side_cols[side].start + start + width)
-            nc.vector.quantize_mx(out=out_codes[:, cols].bitcast(FP8X4), scales=out_scales[:, cols], in_=grouped[:])
-
         words_out = out_1[0].rearrange("p t i -> p (t i)").bitcast(I32)
-        for c in range(0, T, STORE_WIDTH):
-            nc.sync.dma_start(words_out[:, c : c + STORE_WIDTH], out_codes[:, c : c + STORE_WIDTH])
+        for cols, side, pairs, grouped in pieces:
+            weave_words((nc.vector.tensor_copy, nc.scalar.copy)[side], (I32, U32)[side], grouped, pairs)
+        for cols, side, pairs, grouped in pieces:
+            nc.vector.quantize_mx(out=out_codes[:, cols].bitcast(FP8X4), scales=out_scales[:, cols], in_=grouped[:])
+            nc.sync.dma_start(words_out[:, cols], out_codes[:, cols])
         for quad in range(QUADS):
             nc.scalar.dma_start(
                 out_2[0, 4 * quad : 4 * quad + 4, :].bitcast(I32), out_scales[32 * quad : 32 * quad + 4, :].bitcast(I32)

@@ -28,6 +28,8 @@ QUARTER = J // 4
 PER_COL = 16
 RUN = 4
 MOVED_ROWS = 112
+R_SLOTS = ("w_raw0", "words00", "words10", "w_raw2")
+SHARED_AT = {"act0": 0, "h_pairs0": 4096, "act1": 1024, "rw2": 5120}
 OUT_PIECES = ((512, 0), (512, 0), (512, 1), (256, 1), (256, 1))
 
 
@@ -38,9 +40,12 @@ def tile_list_msg_gelu_res_resLP_kernel(
     nc = tc.nc
     with ExitStack() as ctx:
         sb = ctx.enter_context(tc.tile_pool(name="sb", bufs=1))
+        shared = ctx.enter_context(tc.tile_pool(name="shared", bufs=1))
         ps = ctx.enter_context(tc.psum_pool(name="ps", bufs=1))
 
         def sbuf(shape, dtype, name, slot=None):
+            if name in SHARED_AT:
+                return shared.tile(shape, dtype, name=name, offset=SHARED_AT[name], align_bytes=64)
             return sb.tile(shape, dtype, name=name, tag=slot or name, align_bytes=64)
 
         def bank(shape, name, index):
@@ -61,19 +66,14 @@ def tile_list_msg_gelu_res_resLP_kernel(
         tab_sc = sbuf([P, T], U8, "tab_sc")
         nc.gpsimd.memset(tab_sc[:].bitcast(I32), 0)
         wgo_rows = sbuf([P, P], F32, "wgo_rows")
-        nc.gpsimd.memset(wgo_rows[:], 0.0)
+        nc.vector.memset(wgo_rows[:], 0.0)
         ident = sbuf([P, P], F32, "ident")
         make_identity(nc, ident[:])
         wd_sc = sbuf([P, 2 * N], U8, "wd_sc")
-        nc.gpsimd.memset(wd_sc[:].bitcast(I32), 0)
+        nc.vector.memset(wd_sc[:].bitcast(I32), 0)
         moved_sc = sbuf([P, 2 * J], U8, "moved_sc")
         nc.gpsimd.memset(moved_sc[:].bitcast(I32), 0)
         page = [sbuf([P, T], F32, "page%d" % t) for t in range(PACK)]
-        for t in range(2):
-            nc.vector.memset(page[t][:].bitcast(I32), 0)
-        for t in range(2, PACK):
-            for c in range(0, T, T // 4):
-                nc.gpsimd.memset(page[t][:, c : c + T // 4], 0.0)
 
         lists = [sbuf([P, J // PER_COL], U16, "list%d" % s) for s in range(2)]
         tab = sbuf([P, T], I32, "tab")
@@ -90,24 +90,32 @@ def tile_list_msg_gelu_res_resLP_kernel(
                 tab_sc[32 * quad : 32 * quad + 8, :].bitcast(I32),
                 tab_scales[:, 4 * quad : 4 * quad + 4, :].bitcast(I32),
             )
+        nc.sync.dma_start(wgo_rows[0 : J // P, :], wgo[0].rearrange("(b c) -> b c", c=P))
         load_weight(0)
         nc.sync.dma_start(lists[1][:], offs2)
         nc.sync.dma_start(tab[:], tab_words[0].rearrange("p t i -> p (t i)").bitcast(I32))
-        nc.sync.dma_start(wgo_rows[0 : J // P, :], wgo[0].rearrange("(b c) -> b c", c=P))
-        for i in range(1, 4):
-            load_weight(i)
-        wd4 = sbuf([P, 2 * N], U8, "wd4")
-        nc.sync.dma_start(wd4[:].bitcast(I32), wd4_words[0].bitcast(I32))
-        wd8 = sbuf([P, N], I32, "wd8")
-        nc.sync.dma_start(wd8[:], wd8_words[0].rearrange("p n i -> p (n i)").bitcast(I32))
         sm_sb = sbuf([P, PACK], F32, "sm_sb")
-        nc.gpsimd.dma_start(sm_sb[:], sm.rearrange("(p t) -> p t", t=PACK))
-        for i, hbm_scales in enumerate((wd4_scales, wd8_scales)):
+        wd4 = sbuf([P, 2 * N], U8, "wd4")
+        wd8 = sbuf([P, N], I32, "wd8")
+
+        def load_wd_scales(i):
             for quad in range(QUADS):
-                nc.gpsimd.dma_start(
+                nc.sync.dma_start(
                     wd_sc[32 * quad : 32 * quad + 4, N * i : N * (i + 1)].bitcast(I32),
-                    hbm_scales[0, 4 * quad : 4 * quad + 4, :].bitcast(I32),
+                    (wd4_scales, wd8_scales)[i][0, 4 * quad : 4 * quad + 4, :].bitcast(I32),
                 )
+
+        load_weight(1)
+        load_wd_scales(0)
+        load_weight(2)
+        load_wd_scales(1)
+        load_weight(3)
+        nc.sync.dma_start(sm_sb[:], sm.rearrange("(p t) -> p t", t=PACK))
+        nc.sync.dma_start(wd4[:].bitcast(I32), wd4_words[0].bitcast(I32))
+        nc.sync.dma_start(wd8[:], wd8_words[0].rearrange("p n i -> p (n i)").bitcast(I32))
+        for t in range(PACK):
+            for c in range(0, T, T // 4):
+                nc.gpsimd.memset(page[t][:, c : c + T // 4], 0.0)
 
         wgo_col = sbuf([P, J // P], F32, "wgo_col")
         turned = bank([P, P], "wgo_turned", 4)
@@ -155,7 +163,7 @@ def tile_list_msg_gelu_res_resLP_kernel(
             nc.vector.quantize_mx(out=codes[:].bitcast(FP8X4), scales=scales[:], in_=grouped[:])
             w_codes.append(codes)
             w_scales.append(scales)
-            rows = sbuf([P, T], F32, "r_sb%d" % i, "w_raw%d" % i)
+            rows = sbuf([P, T], F32, "r_sb%d" % i, R_SLOTS[i])
             nc.sync.dma_start(rows[:], r_rows[:, i, :])
             r_sb.append(rows)
 
@@ -183,10 +191,8 @@ def tile_list_msg_gelu_res_resLP_kernel(
             quantise_weight(i)
             for t in range(PACK):
                 first_layer(0, t, i)
-            if i == 0:
-                part_words(0, 1, pick_words(0, 1))
-            if i == 1:
-                part_words(1, 1, pick_words(1, 1, "w_grouped1"))
+            if i % 2 == 1:
+                part_words(i // 2, 1, pick_words(i // 2, 1, "w_raw%d" % i))
 
         rw = []
 
@@ -195,24 +201,33 @@ def tile_list_msg_gelu_res_resLP_kernel(
             nc.vector.tensor_tensor(picked[:], r_sb[t][:].indirect(lists[1][:]), wgo_sb[:], MULT)
             rw.append(picked)
 
-        act = [sbuf([P, PACK, HALF], F32, "act%d" % h) for h in range(2)]
+        act = {}
         h_codes, h_scales, y_sb, z_low = {}, {}, {}, {}
-        z2 = [sbuf([P, HALF], F32, "z2_%d" % h) for h in range(2)]
         z3 = sbuf([P, J], F32, "z3")
 
-        def gelu(h, t):
-            nc.scalar.activation(act[h][:, t, :], acc[h, t][:], GELU)
+        def gelu_quarter(q):
+            act[q] = sbuf([P, PACK, QUARTER], F32, "act%d" % q, "act0")
+            for t in range(PACK):
+                nc.scalar.activation(act[q][:, t, :], acc[0, t][:, QUARTER * q : QUARTER * (q + 1)], GELU)
+
+        late_act = sbuf([P, PACK, HALF], F32, "late_act")
+        for c in range(2):
+            act[2 + c] = late_act[:, :, QUARTER * c : QUARTER * (c + 1)]
+
+        def second_half(t):
+            for i in range(4):
+                first_layer(1, t, i)
+            nc.scalar.activation(late_act[:, t, :], acc[1, t][:], GELU)
 
         def hidden(q):
-            h, c = divmod(q, 2)
             pairs = sbuf([P, PACK * QUARTER], BF16, "h_pairs%d" % q)
             for t in range(PACK):
                 nc.scalar.activation(
-                    pair_slot(pairs, t), act[h][:, t, QUARTER * c : QUARTER * (c + 1)], COPY, scale=sm_sb[:, t : t + 1]
+                    pair_slot(pairs, t), act[q][:, t, :], COPY, scale=sm_sb[:, t : t + 1]
                 )
             grouped = sbuf([P, PACK * QUARTER], BF16, "h_grouped%d" % q)
             weave_words(nc.scalar.copy, U32, grouped, pairs)
-            h_codes[q] = sbuf([P, QUARTER], U32, "h_codes%d" % q)
+            h_codes[q] = sbuf([P, QUARTER], U32, "h_codes%d" % q, R_SLOTS[1] if q == 0 else None)
             h_scales[q] = sbuf([P, QUARTER], U8, "h_scales%d" % q)
             nc.vector.quantize_mx(out=h_codes[q][:].bitcast(FP8X4), scales=h_scales[q][:], in_=grouped[:])
 
@@ -249,53 +264,55 @@ def tile_list_msg_gelu_res_resLP_kernel(
             for t in range(2):
                 scatter(t, QUARTER * q, QUARTER, z_low[q][:, t, :])
 
-        def turn_high(h, t, index, dest):
-            z_ps = bank([P, HALF], "z_high_ps%d%d" % (h, t), index)
-            for b in range(PACK):
-                nc.tensor.transpose(z_ps[:, P * b : P * (b + 1)], y_sb[PACK * h + b][:, t, :], ident[:])
+        def turn_high(t, first_block, blocks, index, dest):
+            z_ps = bank([P, P * blocks], "z_high_ps%d%d" % (t, first_block), index)
+            for b in range(blocks):
+                nc.tensor.transpose(z_ps[:, P * b : P * (b + 1)], y_sb[first_block + b][:, t, :], ident[:])
             nc.scalar.copy(dest, z_ps[:])
+
+        def place_third(first_block, blocks, index, slot=None):
+            z = sbuf([P, P * blocks], F32, "z2_%d" % first_block, slot)
+            turn_high(2, first_block, blocks, index, z[:])
+            scatter(2, P * first_block, P * blocks, z[:])
 
         def scatter(t, first, count, z):
             nc.vector.tensor_tensor(
                 page[t][:].indirect(entries(lists[1], first, count)), z, rw[t][:, first : first + count], ADD
             )
 
-        for t in range(3):
+        for t in range(2):
             pick_residual(t)
-        for t in range(PACK):
-            gelu(0, t)
+        gelu_quarter(0)
         hidden(0)
-        pick_residual(3, "h_pairs0")
+        pick_residual(2)
+        pick_residual(3)
+        gelu_quarter(1)
         hidden(1)
-        for t in range(PACK):
-            for i in range(4):
-                first_layer(1, t, i)
         second_layer(0)
-        gelu(1, 0)
+        second_half(0)
         turn_low(0)
-        gelu(1, 1)
         second_layer(1)
-        gelu(1, 2)
+        second_half(1)
         turn_low(1)
-        gelu(1, 3)
+        second_half(2)
+        second_half(3)
         hidden(2)
-        turn_high(0, 2, 7, z2[0][:])
-        scatter(2, 0, HALF, z2[0][:])
+        place_third(0, 2, 7, "h_pairs2")
         hidden(3)
+        place_third(2, 2, 3, "h_pairs3")
         second_layer(2)
-        turn_high(0, 3, 0, z3[:, 0:HALF])
+        turn_high(3, 0, 4, 0, z3[:, 0:HALF])
         turn_low(2)
         second_layer(3)
         turn_low(3)
-        turn_high(1, 2, 1, z2[1][:])
-        scatter(2, HALF, HALF, z2[1][:])
-        turn_high(1, 3, 2, z3[:, HALF:J])
+        place_third(4, 4, 1)
+        turn_high(3, 4, 4, 2, z3[:, HALF:J])
         scatter(3, 0, J, z3[:])
 
         out_rows = out_0.rearrange("(p t) c -> p t c", t=PACK)
         pieces = []
-        pair_slots = ("w_raw0", "w_raw1", "w_raw2", "w_raw3", "tab")
-        group_slots = ("w_grouped0", "w_grouped1", "w_grouped2", "w_grouped3", "words00")
+        pair_slots = R_SLOTS + ("tab",)
+        group_slots = ("w_grouped0", "w_grouped1", "w_grouped2", "w_grouped3", "w_raw3")
         for n, (width, side) in enumerate(OUT_PIECES):
             start = sum(w for w, s in OUT_PIECES[:n])
             pairs = sbuf([P, PACK * width], BF16, "out_pairs%d" % n, pair_slots[n])

@@ -30,7 +30,7 @@ RUN = 4
 MOVED_ROWS = 112
 R_SLOTS = ("w_raw0", "words00", "words10", "w_raw2")
 SHARED_AT = {"act0": 0, "h_pairs0": 4096, "act1": 1024, "rw2": 5120}
-OUT_PIECES = ((512, 0), (512, 0), (512, 1), (256, 1), (256, 1))
+OUT_PIECES = ((512, 0), (256, 0), (128, 0), (512, 1), (256, 1), (256, 1), (128, 1))
 
 
 def tile_list_msg_gelu_res_resLP_kernel(
@@ -77,18 +77,24 @@ def tile_list_msg_gelu_res_resLP_kernel(
 
         lists = [sbuf([P, J // PER_COL], U16, "list%d" % s) for s in range(2)]
         tab = sbuf([P, T], I32, "tab")
-        w_raw = [sbuf([P, PACK, R], F32, "w_raw%d" % i) for i in range(4)]
+        w_raw = [sbuf([P, PACK, R], F32, "w_raw%d" % i) for i in range(3)]
+        last_raw = [sbuf([P, PACK, R // 2], F32, name) for name in ("last_raw", "w_raw3")]
 
         def load_weight(i):
             a, s = divmod(i, 2)
             rows = (ws, wt)[s][K_PASS * a : K_PASS * (a + 1), :]
-            nc.sync.dma_start(w_raw[i][:], rows.rearrange("(p j) r -> p j r", j=PACK))
+            rows = rows.rearrange("(p j) r -> p j r", j=PACK)
+            if i < 3:
+                nc.sync.dma_start(w_raw[i][:], rows)
+            else:
+                for c in range(2):
+                    nc.sync.dma_start(last_raw[c][:], rows[:, :, R // 2 * c : R // 2 * (c + 1)])
 
         nc.sync.dma_start(lists[0][:], offs)
-        for quad in range(QUADS):
+        for r in range(4):
             nc.sync.dma_start(
-                tab_sc[32 * quad : 32 * quad + 8, :].bitcast(I32),
-                tab_scales[:, 4 * quad : 4 * quad + 4, :].bitcast(I32),
+                tab_sc[r:P:16, :].bitcast(I32),
+                tab_scales.rearrange("a (q r) c -> r q a c", r=4)[r].bitcast(I32),
             )
         nc.sync.dma_start(wgo_rows[0 : J // P, :], wgo[0].rearrange("(b c) -> b c", c=P))
         load_weight(0)
@@ -132,7 +138,7 @@ def tile_list_msg_gelu_res_resLP_kernel(
         picked_sc = sbuf([P, 2 * J], U8, "picked_sc")
         for s in range(2):
             nc.vector.tensor_copy(picked_sc[:, J * s : J * (s + 1)], tab_sc[:].indirect(lists[s][:]))
-        nc.sync.dma_start(moved_sc[0:MOVED_ROWS, :].bitcast(I32), picked_sc[4 : 4 + MOVED_ROWS, :].bitcast(I32))
+        nc.sync.dma_start(moved_sc[0:MOVED_ROWS, :].bitcast(I32), picked_sc[16 : 16 + MOVED_ROWS, :].bitcast(I32))
 
         parted = {}
 
@@ -154,10 +160,13 @@ def tile_list_msg_gelu_res_resLP_kernel(
 
         def quantise_weight(i):
             grouped = sbuf([P, PACK * R], BF16, "w_grouped%d" % i)
-            nc.scalar.copy(
-                grouped[:].rearrange("p (t m j) -> p m j t", t=PACK, j=PACK),
-                w_raw[i][:].rearrange("p j (m t) -> p m j t", t=PACK),
-            )
+            dealt = grouped[:].rearrange("p (t m j) -> p m j t", t=PACK, j=PACK)
+            if i < 3:
+                nc.scalar.copy(dealt, w_raw[i][:].rearrange("p j (m t) -> p m j t", t=PACK))
+            else:
+                halves = [raw[:].rearrange("p j (m t) -> p m j t", t=PACK) for raw in last_raw]
+                nc.vector.tensor_copy(dealt[:, 0 : P // 2], halves[0])
+                nc.scalar.copy(dealt[:, P // 2 : P], halves[1])
             codes = sbuf([P, R], U32, "w_codes%d" % i)
             scales = sbuf([P, R], U8, "w_scales%d" % i)
             nc.vector.quantize_mx(out=codes[:].bitcast(FP8X4), scales=scales[:], in_=grouped[:])
@@ -311,8 +320,8 @@ def tile_list_msg_gelu_res_resLP_kernel(
 
         out_rows = out_0.rearrange("(p t) c -> p t c", t=PACK)
         pieces = []
-        pair_slots = R_SLOTS + ("tab",)
-        group_slots = ("w_grouped0", "w_grouped1", "w_grouped2", "w_grouped3", "w_raw3")
+        pair_slots = R_SLOTS + ("tab", "w_raw1", "last_raw")
+        group_slots = ("w_grouped0", "w_grouped1", "w_grouped2", "w_grouped3", "w_raw3", "parted00", "parted10")
         for n, (width, side) in enumerate(OUT_PIECES):
             start = sum(w for w, s in OUT_PIECES[:n])
             pairs = sbuf([P, PACK * width], BF16, "out_pairs%d" % n, pair_slots[n])
@@ -339,6 +348,6 @@ def tile_list_msg_gelu_res_resLP_kernel(
             nc.vector.quantize_mx(out=out_codes[:, cols].bitcast(FP8X4), scales=out_scales[:, cols], in_=grouped[:])
             nc.sync.dma_start(words_out[:, cols], out_codes[:, cols])
         for quad in range(QUADS):
-            nc.scalar.dma_start(
+            (nc.scalar, nc.sync)[quad % 2].dma_start(
                 out_2[0, 4 * quad : 4 * quad + 4, :].bitcast(I32), out_scales[32 * quad : 32 * quad + 4, :].bitcast(I32)
             )

@@ -26,10 +26,20 @@ QUADS = 4
 HALF = J // 2
 QUARTER = J // 4
 PER_COL = 16
-RUN = 4
 MOVED_ROWS = 112
-R_SLOTS = ("w_raw0", "words00", "words10", "w_raw2")
-SHARED_AT = {"act0": 0, "h_pairs0": 4096, "act1": 1024, "rw2": 5120}
+PASS_ORDER = ((0, 1, 2, 3), (3, 2, 1, 0))
+KIB = 1024
+PLACED_AT = {
+    "w_raw0": 0, "sm_sb": 0, "wd8_sc": 64,
+    "parted0_0": 8 * KIB, "tab_sc": 11 * KIB, "r_sb0": 12 * KIB,
+    "w_raw1": 20 * KIB, "r_sb1": 20 * KIB, "h_codes0": 20 * KIB,
+    "w_raw2": 28 * KIB, "wd4": 28 * KIB, "wd8": 29 * KIB, "r_sb2": 31 * KIB, "act2": 31 * KIB, "act3": 31 * KIB,
+    "w_raw4": 39 * KIB, "parted1_512": 39 * KIB, "w_raw3": 43 * KIB, "words1_512": 43 * KIB, "r_sb3": 45 * KIB,
+    "h_codes1": 45 * KIB, "z0": 46 * KIB, "h_pairs2": 48 * KIB, "z1": 48 * KIB,
+    "h_pairs3": 53 * KIB, "z2": 53 * KIB, "h_grouped3": 55 * KIB, "z_late": 55 * KIB,
+}
+PAIRS_AT = 12 * KIB
+GROUPED_AT = 61 * KIB
 OUT_PIECES = ((512, 0), (256, 0), (128, 0), (512, 1), (256, 1), (256, 1), (128, 1))
 
 
@@ -40,12 +50,13 @@ def tile_list_msg_gelu_res_resLP_kernel(
     nc = tc.nc
     with ExitStack() as ctx:
         sb = ctx.enter_context(tc.tile_pool(name="sb", bufs=1))
-        shared = ctx.enter_context(tc.tile_pool(name="shared", bufs=1))
+        placed = ctx.enter_context(tc.tile_pool(name="placed", bufs=1))
         ps = ctx.enter_context(tc.psum_pool(name="ps", bufs=1))
 
-        def sbuf(shape, dtype, name, slot=None):
-            if name in SHARED_AT:
-                return shared.tile(shape, dtype, name=name, offset=SHARED_AT[name], align_bytes=64)
+        def sbuf(shape, dtype, name, slot=None, at=None):
+            at = PLACED_AT.get(name, at)
+            if at is not None:
+                return placed.tile(shape, dtype, name=name, offset=at, align_bytes=64)
             return sb.tile(shape, dtype, name=name, tag=slot or name, align_bytes=64)
 
         def bank(shape, name, index):
@@ -63,33 +74,24 @@ def tile_list_msg_gelu_res_resLP_kernel(
         def pair_slot(pairs, t):
             return pairs[:].rearrange("p (u c e) -> p u c e", u=2, e=2)[:, t // 2, :, t % 2]
 
+        def load_scale_rows(plane, rows):
+            nc.gpsimd.memset(plane[:].bitcast(I32), 0)
+            for quad in range(QUADS):
+                nc.sync.dma_start(
+                    plane[32 * quad : 32 * quad + 4, :].bitcast(I32), rows[0, 4 * quad : 4 * quad + 4, :].bitcast(I32)
+                )
+
         tab_sc = sbuf([P, T], U8, "tab_sc")
         nc.gpsimd.memset(tab_sc[:].bitcast(I32), 0)
         wgo_rows = sbuf([P, P], F32, "wgo_rows")
         nc.vector.memset(wgo_rows[:], 0.0)
+        moved_sc = sbuf([P, 2 * J], U8, "moved_sc")
+        nc.vector.memset(moved_sc[:].bitcast(I32), 0)
         ident = sbuf([P, P], F32, "ident")
         make_identity(nc, ident[:])
-        wd_sc = sbuf([P, 2 * N], U8, "wd_sc")
-        nc.vector.memset(wd_sc[:].bitcast(I32), 0)
-        moved_sc = sbuf([P, 2 * J], U8, "moved_sc")
-        nc.gpsimd.memset(moved_sc[:].bitcast(I32), 0)
-        page = [sbuf([P, T], F32, "page%d" % t) for t in range(PACK)]
 
         lists = [sbuf([P, J // PER_COL], U16, "list%d" % s) for s in range(2)]
         tab = sbuf([P, T], I32, "tab")
-        w_raw = [sbuf([P, PACK, R], F32, "w_raw%d" % i) for i in range(3)]
-        last_raw = [sbuf([P, PACK, R // 2], F32, name) for name in ("last_raw", "w_raw3")]
-
-        def load_weight(i):
-            a, s = divmod(i, 2)
-            rows = (ws, wt)[s][K_PASS * a : K_PASS * (a + 1), :]
-            rows = rows.rearrange("(p j) r -> p j r", j=PACK)
-            if i < 3:
-                nc.sync.dma_start(w_raw[i][:], rows)
-            else:
-                for c in range(2):
-                    nc.sync.dma_start(last_raw[c][:], rows[:, :, R // 2 * c : R // 2 * (c + 1)])
-
         nc.sync.dma_start(lists[0][:], offs)
         for r in range(4):
             nc.sync.dma_start(
@@ -97,235 +99,236 @@ def tile_list_msg_gelu_res_resLP_kernel(
                 tab_scales.rearrange("a (q r) c -> r q a c", r=4)[r].bitcast(I32),
             )
         nc.sync.dma_start(wgo_rows[0 : J // P, :], wgo[0].rearrange("(b c) -> b c", c=P))
-        load_weight(0)
-        nc.sync.dma_start(lists[1][:], offs2)
         nc.sync.dma_start(tab[:], tab_words[0].rearrange("p t i -> p (t i)").bitcast(I32))
-        sm_sb = sbuf([P, PACK], F32, "sm_sb")
-        wd4 = sbuf([P, 2 * N], U8, "wd4")
-        wd8 = sbuf([P, N], I32, "wd8")
 
-        def load_wd_scales(i):
-            for quad in range(QUADS):
-                nc.sync.dma_start(
-                    wd_sc[32 * quad : 32 * quad + 4, N * i : N * (i + 1)].bitcast(I32),
-                    (wd4_scales, wd8_scales)[i][0, 4 * quad : 4 * quad + 4, :].bitcast(I32),
-                )
+        def weight_rows(i):
+            a, s = divmod(i, 2)
+            return (ws, wt)[s][K_PASS * a : K_PASS * (a + 1), :].rearrange("(p j) r -> p j r", j=PACK)
 
-        load_weight(1)
-        load_wd_scales(0)
-        load_weight(2)
-        load_wd_scales(1)
-        load_weight(3)
-        nc.sync.dma_start(sm_sb[:], sm.rearrange("(p t) -> p t", t=PACK))
-        nc.sync.dma_start(wd4[:].bitcast(I32), wd4_words[0].bitcast(I32))
-        nc.sync.dma_start(wd8[:], wd8_words[0].rearrange("p n i -> p (n i)").bitcast(I32))
-        for t in range(PACK):
-            for c in range(0, T, T // 4):
-                nc.gpsimd.memset(page[t][:, c : c + T // 4], 0.0)
+        w_raw = []
+
+        def load_weight(i, first, count):
+            raw = sbuf([P, PACK, count], F32, "w_raw%d" % len(w_raw))
+            nc.sync.dma_start(raw[:], weight_rows(i)[:, :, first : first + count])
+            w_raw.append(raw)
+
+        load_weight(0, 0, R)
+        nc.sync.dma_start(lists[1][:], offs2)
+        load_weight(1, 0, R)
+        wd4_sc = sbuf([P, N], U8, "wd4_sc")
+        load_scale_rows(wd4_sc, wd4_scales)
+        load_weight(2, 0, R)
+        for c in range(2):
+            load_weight(3, R // 2 * c, R // 2)
 
         wgo_col = sbuf([P, J // P], F32, "wgo_col")
-        turned = bank([P, P], "wgo_turned", 4)
+        turned = bank([P, P], "wgo_turned", 2)
         nc.tensor.transpose(turned[:], wgo_rows[:], ident[:])
+        to_spread = sbuf([P, J // P], F32, "to_spread", "w_grouped0")
+        nc.scalar.copy(to_spread[:], turned[:, 0 : J // P])
         nc.scalar.copy(wgo_col[:], turned[:, 0 : J // P])
         wgo_sb = sbuf([P, J], F32, "wgo_sb")
         for g in range(2):
-            spread = bank([P, PACK, P], "wgo_spread%d" % g, 5 + g)
+            spread = bank([P, PACK, P], "wgo_spread%d" % g, 6 + g)
             for b in range(PACK):
                 col = PACK * g + b
-                nc.tensor.transpose(spread[:, b, :], wgo_col[:, col : col + 1].to_broadcast([P, P]), ident[:])
+                nc.tensor.transpose(spread[:, b, :], to_spread[:, col : col + 1].to_broadcast([P, P]), ident[:])
             nc.scalar.copy(wgo_sb[:, HALF * g : HALF * (g + 1)], spread[:].rearrange("p b c -> p (b c)"))
 
         picked_sc = sbuf([P, 2 * J], U8, "picked_sc")
-        for s in range(2):
-            nc.vector.tensor_copy(picked_sc[:, J * s : J * (s + 1)], tab_sc[:].indirect(lists[s][:]))
-        nc.sync.dma_start(moved_sc[0:MOVED_ROWS, :].bitcast(I32), picked_sc[16 : 16 + MOVED_ROWS, :].bitcast(I32))
-
         parted = {}
 
-        def pick_words(s, h, slot=None):
-            words = sbuf([P, HALF], U32, "words%d%d" % (s, h), slot)
-            nc.vector.tensor_copy(words[:], tab[:].bitcast(U32).indirect(entries(lists[s], HALF * h, HALF)))
+        def pick_words(s, first, count):
+            words = sbuf([P, count], U32, "words%d_%d" % (s, first))
+            nc.vector.tensor_copy(words[:], tab[:].bitcast(U32).indirect(entries(lists[s], first, count)))
             return words
 
-        def part_words(s, h, words):
-            both = sbuf([P, 2 * 2 * HALF], U8, "parted%d%d" % (s, h))
+        def part_words(s, first, count, words):
+            both = sbuf([P, 2, 2 * count], U8, "parted%d_%d" % (s, first))
             nc.vector.tensor_copy(
-                both[:].bitcast(U16).rearrange("p (d j) -> p d j", d=2),
+                both[:].rearrange("p d b -> p (d b)").bitcast(U16).rearrange("p (d j) -> p d j", d=2),
                 words[:].bitcast(U16).rearrange("p (j d) -> p d j", d=2),
             )
-            parted[s, h] = both
+            for q in range(first // QUARTER, (first + count) // QUARTER):
+                parted[s, q] = both[:, :, 2 * (QUARTER * q - first) : 2 * (QUARTER * (q + 1) - first)]
 
-        w_codes, w_scales, r_sb = [], [], []
-        r_rows = rT.rearrange("(p t) c -> p t c", t=PACK)
+        early = []
+        for s, count in ((0, J), (1, HALF)):
+            nc.vector.tensor_copy(picked_sc[:, J * s : J * (s + 1)], tab_sc[:].indirect(lists[s][:]))
+            early.append((s, 0, count, pick_words(s, 0, count)))
+        nc.sync.dma_start(moved_sc[0:MOVED_ROWS, :].bitcast(I32), picked_sc[16 : 16 + MOVED_ROWS, :].bitcast(I32))
+        for job in early:
+            part_words(*job)
+
+        w_codes, w_scales = [], []
 
         def quantise_weight(i):
             grouped = sbuf([P, PACK * R], BF16, "w_grouped%d" % i)
             dealt = grouped[:].rearrange("p (t m j) -> p m j t", t=PACK, j=PACK)
-            if i < 3:
-                nc.scalar.copy(dealt, w_raw[i][:].rearrange("p j (m t) -> p m j t", t=PACK))
-            else:
-                halves = [raw[:].rearrange("p j (m t) -> p m j t", t=PACK) for raw in last_raw]
-                nc.vector.tensor_copy(dealt[:, 0 : P // 2], halves[0])
-                nc.scalar.copy(dealt[:, P // 2 : P], halves[1])
+            raws = w_raw[i:] if i == 3 else w_raw[i : i + 1]
+            for c, raw in enumerate(raws):
+                part = P // len(raws)
+                nc.scalar.copy(dealt[:, part * c : part * (c + 1)], raw[:].rearrange("p j (m t) -> p m j t", t=PACK))
             codes = sbuf([P, R], U32, "w_codes%d" % i)
             scales = sbuf([P, R], U8, "w_scales%d" % i)
             nc.vector.quantize_mx(out=codes[:].bitcast(FP8X4), scales=scales[:], in_=grouped[:])
             w_codes.append(codes)
             w_scales.append(scales)
-            rows = sbuf([P, T], F32, "r_sb%d" % i, R_SLOTS[i])
-            nc.sync.dma_start(rows[:], r_rows[:, i, :])
-            r_sb.append(rows)
 
         acc = {}
 
-        def first_layer(h, t, i):
+        def first_layer(q, t, i):
             a, s = divmod(i, 2)
-            if i == 0:
-                acc[h, t] = bank([P, HALF], "acc%d%d" % (h, t), t)
-            first = J * s + HALF * h
+            b, u = divmod(t, 2)
+            order = PASS_ORDER[min(q, 1)]
+            if i == order[0] and u == 0:
+                acc[q, b] = bank([P, 2, QUARTER], "acc%d%d" % (q, b), 6 * (q % 2) + b)
+            first = J * s + QUARTER * q
             nc.tensor.matmul_mx(
-                out=acc[h, t][:],
+                out=acc[q, b][:, u, :],
                 lhsT=w_codes[i][:, P * t : P * (t + 1)].bitcast(FP8X4),
                 lhsT_scale=w_scales[i][:, P * t : P * (t + 1)],
-                rhs=parted[s, h][:, 2 * HALF * a : 2 * HALF * (a + 1)].bitcast(FP4X4),
-                rhs_scale=(picked_sc, moved_sc)[a][:, first : first + HALF],
-                start=(i == 0),
-                stop=(i == 3),
+                rhs=parted[s, q][:, a, :].bitcast(FP4X4),
+                rhs_scale=(picked_sc, moved_sc)[a][:, first : first + QUARTER],
+                start=(i == order[0] and u == 0),
+                stop=(i == order[3] and u == 1),
             )
 
-        first_words = [pick_words(s, 0) for s in range(2)]
-        for s in range(2):
-            part_words(s, 0, first_words[s])
+        r_rows = rT.rearrange("(p t) c -> p t c", t=PACK)
+        r_sb = []
+
+        def load_residual(n):
+            rows = sbuf([P, T], F32, "r_sb%d" % n)
+            nc.sync.dma_start(rows[:], r_rows[:, PACK - 1 - n, :])
+            r_sb.append(rows)
+
         for i in range(4):
             quantise_weight(i)
             for t in range(PACK):
                 first_layer(0, t, i)
-            if i % 2 == 1:
-                part_words(i // 2, 1, pick_words(i // 2, 1, "w_raw%d" % i))
 
-        rw = []
+        part_words(1, HALF, HALF, pick_words(1, HALF, HALF))
+        load_residual(0)
+        wd8_sc = sbuf([P, N], U8, "wd8_sc")
+        load_scale_rows(wd8_sc, wd8_scales)
+        sm_sb = sbuf([P, PACK], F32, "sm_sb")
+        nc.sync.dma_start(sm_sb[:], sm.rearrange("(p t) -> p t", t=PACK))
+        load_residual(1)
+        wd4 = sbuf([P, 2 * N], U8, "wd4")
+        wd8 = sbuf([P, N], I32, "wd8")
+        nc.sync.dma_start(wd4[:].bitcast(I32), wd4_words[0].bitcast(I32))
+        nc.sync.dma_start(wd8[:], wd8_words[0].rearrange("p n i -> p (n i)").bitcast(I32))
+        load_residual(2)
+        load_residual(3)
 
-        def pick_residual(t, slot=None):
-            picked = sbuf([P, J], F32, "rw%d" % t, slot)
-            nc.vector.tensor_tensor(picked[:], r_sb[t][:].indirect(lists[1][:]), wgo_sb[:], MULT)
-            rw.append(picked)
+        page = [sbuf([P, T], F32, "page%d" % t) for t in range(PACK)]
+        for t in range(PACK):
+            for c in range(0, T, T // 4):
+                nc.gpsimd.memset(page[t][:, c : c + T // 4], 0.0)
 
-        act = {}
-        h_codes, h_scales, y_sb, z_low = {}, {}, {}, {}
-        z3 = sbuf([P, J], F32, "z3")
+        rw = {}
 
-        def gelu_quarter(q):
-            act[q] = sbuf([P, PACK, QUARTER], F32, "act%d" % q, "act0")
-            for t in range(PACK):
-                nc.scalar.activation(act[q][:, t, :], acc[0, t][:, QUARTER * q : QUARTER * (q + 1)], GELU)
+        def pick_residual(n):
+            t = PACK - 1 - n
+            rw[t] = sbuf([P, J], F32, "rw%d" % t)
+            nc.vector.tensor_tensor(rw[t][:], r_sb[n][:].indirect(lists[1][:]), wgo_sb[:], MULT)
 
-        late_act = sbuf([P, PACK, HALF], F32, "late_act")
-        for c in range(2):
-            act[2 + c] = late_act[:, :, QUARTER * c : QUARTER * (c + 1)]
+        act, h_codes, h_scales, y_sb = {}, {}, {}, {}
 
-        def second_half(t):
-            for i in range(4):
-                first_layer(1, t, i)
-            nc.scalar.activation(late_act[:, t, :], acc[1, t][:], GELU)
+        def gelu(q):
+            if q > 0:
+                for t in range(PACK):
+                    for i in PASS_ORDER[1]:
+                        first_layer(q, t, i)
+            act[q] = sbuf([P, PACK, QUARTER], F32, "act%d" % q, "act")
+            for b in range(2):
+                nc.scalar.activation(act[q][:, 2 * b : 2 * b + 2, :], acc[q, b][:], GELU)
 
         def hidden(q):
             pairs = sbuf([P, PACK * QUARTER], BF16, "h_pairs%d" % q)
             for t in range(PACK):
-                nc.scalar.activation(
-                    pair_slot(pairs, t), act[q][:, t, :], COPY, scale=sm_sb[:, t : t + 1]
-                )
+                nc.scalar.activation(pair_slot(pairs, t), act[q][:, t, :], COPY, scale=sm_sb[:, t : t + 1])
             grouped = sbuf([P, PACK * QUARTER], BF16, "h_grouped%d" % q)
             weave_words(nc.scalar.copy, U32, grouped, pairs)
-            h_codes[q] = sbuf([P, QUARTER], U32, "h_codes%d" % q, R_SLOTS[1] if q == 0 else None)
+            h_codes[q] = sbuf([P, QUARTER], U32, "h_codes%d" % q)
             h_scales[q] = sbuf([P, QUARTER], U8, "h_scales%d" % q)
             nc.vector.quantize_mx(out=h_codes[q][:].bitcast(FP8X4), scales=h_scales[q][:], in_=grouped[:])
 
         def second_layer(q):
             for b in range(2):
                 cols = slice(P * b, P * (b + 1))
-                y_ps = bank([P, N], "y_ps%d%d" % (q, b), 4 + b)
-                for i, (words, fmt) in enumerate(((wd4, FP4X4), (wd8, FP8X4))):
+                y_ps = bank([P, N], "y_ps%d%d" % (q, b), 2 + b)
+                for i, (packed, plane, fmt) in enumerate(((wd4, wd4_sc, FP4X4), (wd8, wd8_sc, FP8X4))):
                     nc.tensor.matmul_mx(
                         out=y_ps[:],
                         lhsT=h_codes[q][:, cols].bitcast(FP8X4),
                         lhsT_scale=h_scales[q][:, cols],
-                        rhs=words[:].bitcast(fmt),
-                        rhs_scale=wd_sc[:, N * i : N * (i + 1)],
+                        rhs=packed[:].bitcast(fmt),
+                        rhs_scale=plane[:],
                         start=(i == 0),
                         stop=(i == 1),
                     )
+                y_sb[q, b] = sbuf([P, PACK, P], F32, "y_sb%d%d" % (q, b))
                 block = 2 * q + b
-                y_sb[block] = sbuf([P, PACK, P], F32, "y_sb%d" % block)
                 nc.scalar.activation(
-                    y_sb[block][:],
+                    y_sb[q, b][:],
                     y_ps[:].rearrange("j (p t) -> j t p", t=PACK),
                     COPY,
                     scale=wgo_col[:, block : block + 1],
                 )
 
-        def turn_low(q):
-            z_ps = bank([P, 2, QUARTER], "z_low_ps%d" % q, 6)
-            for b in range(2):
-                for t in range(2):
-                    nc.tensor.transpose(z_ps[:, t, P * b : P * (b + 1)], y_sb[2 * q + b][:, t, :], ident[:])
-            z_low[q] = sbuf([P, 2, QUARTER], F32, "z_low%d" % q)
-            nc.scalar.copy(z_low[q][:], z_ps[:])
-            for t in range(2):
-                scatter(t, QUARTER * q, QUARTER, z_low[q][:, t, :])
+        def turn(z, place, units, index):
+            z_ps = bank([P, len(units) * QUARTER], "z_ps%d%d" % units[0], index)
+            for n, (t, q) in enumerate(units):
+                for b in range(2):
+                    first = QUARTER * n + P * b
+                    nc.tensor.transpose(z_ps[:, first : first + P], y_sb[q, b][:, t, :], ident[:])
+            nc.scalar.copy(z[:, place : place + len(units) * QUARTER], z_ps[:])
 
-        def turn_high(t, first_block, blocks, index, dest):
-            z_ps = bank([P, P * blocks], "z_high_ps%d%d" % (t, first_block), index)
-            for b in range(blocks):
-                nc.tensor.transpose(z_ps[:, P * b : P * (b + 1)], y_sb[first_block + b][:, t, :], ident[:])
-            nc.scalar.copy(dest, z_ps[:])
-
-        def place_third(first_block, blocks, index, slot=None):
-            z = sbuf([P, P * blocks], F32, "z2_%d" % first_block, slot)
-            turn_high(2, first_block, blocks, index, z[:])
-            scatter(2, P * first_block, P * blocks, z[:])
-
-        def scatter(t, first, count, z):
+        def scatter(t, first_quarter, quarters, z):
+            first, count = QUARTER * first_quarter, QUARTER * quarters
             nc.vector.tensor_tensor(
                 page[t][:].indirect(entries(lists[1], first, count)), z, rw[t][:, first : first + count], ADD
             )
 
-        for t in range(2):
-            pick_residual(t)
-        gelu_quarter(0)
+        def place(name, q, groups):
+            sets = [t for group in groups for t in group]
+            z = sbuf([P, len(sets) * QUARTER], F32, name)
+            for n, group in enumerate(groups):
+                turn(z, QUARTER * sets.index(group[0]), [(t, q) for t in group], 4 + (n + group[0]) % 2)
+            for n, t in enumerate(sets):
+                scatter(t, q, 1, z[:, QUARTER * n : QUARTER * (n + 1)])
+
+        pick_residual(0)
+        pick_residual(1)
+        gelu(0)
         hidden(0)
         pick_residual(2)
         pick_residual(3)
-        gelu_quarter(1)
-        hidden(1)
-        second_layer(0)
-        second_half(0)
-        turn_low(0)
-        second_layer(1)
-        second_half(1)
-        turn_low(1)
-        second_half(2)
-        second_half(3)
-        hidden(2)
-        place_third(0, 2, 7, "h_pairs2")
-        hidden(3)
-        place_third(2, 2, 3, "h_pairs3")
-        second_layer(2)
-        turn_high(3, 0, 4, 0, z3[:, 0:HALF])
-        turn_low(2)
-        second_layer(3)
-        turn_low(3)
-        place_third(4, 4, 1)
-        turn_high(3, 4, 4, 2, z3[:, HALF:J])
-        scatter(3, 0, J, z3[:])
+        for q in range(4):
+            if q < 3:
+                gelu(q + 1)
+            second_layer(q)
+            if q < 3:
+                hidden(q + 1)
+            if q == 0:
+                place("z_first", 0, [[0]])
+                place("z0", 0, [[1, 2]])
+            else:
+                place("z%d" % q, q, [[0, 1], [2]] if q == 1 else [[0, 1]])
+        z_late = sbuf([P, HALF + J], F32, "z_late")
+        turn(z_late, 0, [(2, 2), (2, 3)], 5)
+        scatter(2, 2, 2, z_late[:, 0:HALF])
+        for h in range(2):
+            turn(z_late, HALF * (h + 1), [(3, 2 * h), (3, 2 * h + 1)], h)
+        scatter(3, 0, 4, z_late[:, HALF : HALF + J])
 
         out_rows = out_0.rearrange("(p t) c -> p t c", t=PACK)
         pieces = []
-        pair_slots = R_SLOTS + ("tab", "w_raw1", "last_raw")
-        group_slots = ("w_grouped0", "w_grouped1", "w_grouped2", "w_grouped3", "w_raw3", "parted00", "parted10")
         for n, (width, side) in enumerate(OUT_PIECES):
             start = sum(w for w, s in OUT_PIECES[:n])
-            pairs = sbuf([P, PACK * width], BF16, "out_pairs%d" % n, pair_slots[n])
-            grouped = sbuf([P, PACK * width], BF16, "out_grouped%d" % n, group_slots[n])
+            pairs = sbuf([P, PACK * width], BF16, "out_pairs%d" % n, at=PAIRS_AT + 2 * PACK * start)
+            grouped = sbuf([P, PACK * width], BF16, "out_grouped%d" % n, at=GROUPED_AT + 2 * PACK * start)
             pieces.append((slice(start, start + width), side, pairs, grouped))
         for t in range(PACK):
             nc.sync.dma_start(out_rows[:, t, :], page[t][:])

@@ -28,10 +28,16 @@ QUARTER = J // 4
 PER_COL = 16
 MOVED_ROWS = 112
 PASS_ORDER = ((0, 1, 2, 3), (3, 2, 1, 0))
+EARLY_UNITS = (
+    [[(1, 0, 2), (2, 0, 2)]],
+    [[(3, 0, 2)], [(0, 2, 2), (1, 2, 2)]],
+    [[(0, 4, 2)], [(1, 4, 2)]],
+    [[(0, 6, 1), (1, 6, 1)], [(0, 7, 1), (1, 7, 1)]],
+)
 KIB = 1024
 PLACED_AT = {
     "w_raw0": 0, "sm_sb": 0, "wd8_sc": 64,
-    "parted0_0": 8 * KIB, "tab_sc": 11 * KIB, "r_sb0": 12 * KIB,
+    "words0_0": 8 * KIB, "w_codes0": 8 * KIB, "tab_sc": 12 * KIB, "r_sb0": 12 * KIB,
     "w_raw1": 20 * KIB, "r_sb1": 20 * KIB, "h_codes0": 20 * KIB,
     "w_raw2": 28 * KIB, "wd4": 28 * KIB, "wd8": 29 * KIB, "r_sb2": 31 * KIB, "act2": 31 * KIB, "act3": 31 * KIB,
     "w_raw4": 39 * KIB, "parted1_512": 39 * KIB, "w_raw3": 43 * KIB, "words1_512": 43 * KIB, "r_sb3": 45 * KIB,
@@ -40,7 +46,8 @@ PLACED_AT = {
 }
 PAIRS_AT = 12 * KIB
 GROUPED_AT = 61 * KIB
-OUT_PIECES = ((512, 0), (256, 0), (128, 0), (512, 1), (256, 1), (256, 1), (128, 1))
+OUT_TILES = ((0, (512,)), (0, (384,)), (1, (512,)), (1, (256,)), (1, (256, 128)))
+OVERLAP = 8
 
 
 def tile_list_msg_gelu_res_resLP_kernel(
@@ -99,7 +106,7 @@ def tile_list_msg_gelu_res_resLP_kernel(
                 tab_scales.rearrange("a (q r) c -> r q a c", r=4)[r].bitcast(I32),
             )
         nc.sync.dma_start(wgo_rows[0 : J // P, :], wgo[0].rearrange("(b c) -> b c", c=P))
-        nc.sync.dma_start(tab[:], tab_words[0].rearrange("p t i -> p (t i)").bitcast(I32))
+        nc.sync.dma_start(lists[1][:], offs2)
 
         def weight_rows(i):
             a, s = divmod(i, 2)
@@ -113,7 +120,7 @@ def tile_list_msg_gelu_res_resLP_kernel(
             w_raw.append(raw)
 
         load_weight(0, 0, R)
-        nc.sync.dma_start(lists[1][:], offs2)
+        nc.sync.dma_start(tab[:], tab_words[0].rearrange("p t i -> p (t i)").bitcast(I32))
         load_weight(1, 0, R)
         wd4_sc = sbuf([P, N], U8, "wd4_sc")
         load_scale_rows(wd4_sc, wd4_scales)
@@ -152,10 +159,9 @@ def tile_list_msg_gelu_res_resLP_kernel(
             for q in range(first // QUARTER, (first + count) // QUARTER):
                 parted[s, q] = both[:, :, 2 * (QUARTER * q - first) : 2 * (QUARTER * (q + 1) - first)]
 
-        early = []
-        for s, count in ((0, J), (1, HALF)):
+        for s in range(2):
             nc.vector.tensor_copy(picked_sc[:, J * s : J * (s + 1)], tab_sc[:].indirect(lists[s][:]))
-            early.append((s, 0, count, pick_words(s, 0, count)))
+        early = [(s, 0, count, pick_words(s, 0, count)) for s, count in ((0, J), (1, HALF))]
         nc.sync.dma_start(moved_sc[0:MOVED_ROWS, :].bitcast(I32), picked_sc[16 : 16 + MOVED_ROWS, :].bitcast(I32))
         for job in early:
             part_words(*job)
@@ -278,26 +284,29 @@ def tile_list_msg_gelu_res_resLP_kernel(
                 )
 
         def turn(z, place, units, index):
-            z_ps = bank([P, len(units) * QUARTER], "z_ps%d%d" % units[0], index)
-            for n, (t, q) in enumerate(units):
-                for b in range(2):
-                    first = QUARTER * n + P * b
-                    nc.tensor.transpose(z_ps[:, first : first + P], y_sb[q, b][:, t, :], ident[:])
-            nc.scalar.copy(z[:, place : place + len(units) * QUARTER], z_ps[:])
+            width = P * sum(unit[2] for unit in units)
+            z_ps = bank([P, width], "z_ps%d%d" % units[0][0:2], index)
+            first = 0
+            for t, first_block, blocks in units:
+                for block in range(first_block, first_block + blocks):
+                    nc.tensor.transpose(z_ps[:, first : first + P], y_sb[divmod(block, 2)][:, t, :], ident[:])
+                    first = first + P
+            nc.scalar.copy(z[:, place : place + width], z_ps[:])
 
-        def scatter(t, first_quarter, quarters, z):
-            first, count = QUARTER * first_quarter, QUARTER * quarters
+        def scatter(t, first_block, blocks, z):
+            first, count = P * first_block, P * blocks
             nc.vector.tensor_tensor(
                 page[t][:].indirect(entries(lists[1], first, count)), z, rw[t][:, first : first + count], ADD
             )
 
-        def place(name, q, groups):
-            sets = [t for group in groups for t in group]
-            z = sbuf([P, len(sets) * QUARTER], F32, name)
+        def place(name, groups):
+            z = sbuf([P, P * sum(unit[2] for group in groups for unit in group)], F32, name)
+            first = 0
             for n, group in enumerate(groups):
-                turn(z, QUARTER * sets.index(group[0]), [(t, q) for t in group], 4 + (n + group[0]) % 2)
-            for n, t in enumerate(sets):
-                scatter(t, q, 1, z[:, QUARTER * n : QUARTER * (n + 1)])
+                turn(z, first, group, 4 + n % 2)
+                for unit in group:
+                    scatter(*unit, z[:, first : first + P * unit[2]])
+                    first = first + P * unit[2]
 
         pick_residual(0)
         pick_residual(1)
@@ -312,45 +321,54 @@ def tile_list_msg_gelu_res_resLP_kernel(
             if q < 3:
                 hidden(q + 1)
             if q == 0:
-                place("z_first", 0, [[0]])
-                place("z0", 0, [[1, 2]])
-            else:
-                place("z%d" % q, q, [[0, 1], [2]] if q == 1 else [[0, 1]])
-        z_late = sbuf([P, HALF + J], F32, "z_late")
-        turn(z_late, 0, [(2, 2), (2, 3)], 5)
-        scatter(2, 2, 2, z_late[:, 0:HALF])
-        for h in range(2):
-            turn(z_late, HALF * (h + 1), [(3, 2 * h), (3, 2 * h + 1)], h)
-        scatter(3, 0, 4, z_late[:, HALF : HALF + J])
+                place("z_first", [[(0, 0, 2)]])
+            place("z%d" % q, EARLY_UNITS[q])
+        z_late = sbuf([P, 2, 3 * QUARTER], F32, "z_late")
+        for e in range(2):
+            turn(z_late[:, e, :], 0, [(2 + e, 2, 4)], e)
+            turn(z_late[:, e, :], HALF, [(2 + e, 6, 2)], 6 + e)
+            scatter(2 + e, 2, 6, z_late[:, e, :])
 
         out_rows = out_0.rearrange("(p t) c -> p t c", t=PACK)
-        pieces = []
-        for n, (width, side) in enumerate(OUT_PIECES):
-            start = sum(w for w, s in OUT_PIECES[:n])
-            pairs = sbuf([P, PACK * width], BF16, "out_pairs%d" % n, at=PAIRS_AT + 2 * PACK * start)
-            grouped = sbuf([P, PACK * width], BF16, "out_grouped%d" % n, at=GROUPED_AT + 2 * PACK * start)
-            pieces.append((slice(start, start + width), side, pairs, grouped))
+        tiles = []
+        for n, (side, widths) in enumerate(OUT_TILES):
+            start = sum(sum(w) for s, w in OUT_TILES[:n])
+            pairs = sbuf([P, PACK * sum(widths)], BF16, "out_pairs%d" % n, at=PAIRS_AT + 2 * PACK * start)
+            tiles.append((start, side, widths, pairs))
         for t in range(PACK):
             nc.sync.dma_start(out_rows[:, t, :], page[t][:])
-            for cols, side, pairs, grouped in pieces:
+            for start, side, widths, pairs in tiles:
+                width = sum(widths)
                 if side == 0 and t == 2:
-                    width = cols.stop - cols.start
+                    whole = width - OVERLAP
+                    nc.scalar.copy(pair_slot(pairs, t)[:, 0:whole], page[t][:, start : start + whole])
                     nc.scalar.copy(
-                        pairs[:].rearrange("p (u c e) -> p u c e", u=2, e=2)[:, 1, :, :],
-                        page[t][:, cols].unsqueeze(2).to_broadcast([P, width, 2]),
+                        pairs[:].rearrange("p (u c e) -> p u c e", u=2, e=2)[:, 1, whole:width, :],
+                        page[t][:, start + whole : start + width].unsqueeze(2).to_broadcast([P, OVERLAP, 2]),
                     )
                 else:
                     copy = nc.vector.tensor_copy if (t == 3 and side == 0) else nc.scalar.copy
-                    copy(pair_slot(pairs, t), page[t][:, cols])
+                    copy(pair_slot(pairs, t), page[t][:, start : start + width])
         out_codes = sbuf([P, T], I32, "out_codes")
         out_scales = sbuf([P, T], U8, "out_scales")
         words_out = out_1[0].rearrange("p t i -> p (t i)").bitcast(I32)
-        for cols, side, pairs, grouped in pieces:
-            weave_words((nc.vector.tensor_copy, nc.scalar.copy)[side], (I32, U32)[side], grouped, pairs)
-        for cols, side, pairs, grouped in pieces:
+        pieces = []
+        for start, side, widths, pairs in tiles:
+            copy, dtype = ((nc.vector.tensor_copy, I32), (nc.scalar.copy, U32))[side]
+            first = 0
+            for width in widths:
+                at = GROUPED_AT + 2 * PACK * (start + first)
+                grouped = sbuf([P, PACK * width], BF16, "out_grouped%d" % len(pieces), at=at)
+                copy(
+                    grouped[:].bitcast(dtype).rearrange("p (c u) -> p c u", u=2),
+                    pairs[:].bitcast(dtype).rearrange("p (u c) -> p c u", u=2)[:, first : first + width, :],
+                )
+                pieces.append((slice(start + first, start + first + width), grouped))
+                first = first + width
+        for cols, grouped in pieces:
             nc.vector.quantize_mx(out=out_codes[:, cols].bitcast(FP8X4), scales=out_scales[:, cols], in_=grouped[:])
             nc.sync.dma_start(words_out[:, cols], out_codes[:, cols])
         for quad in range(QUADS):
-            (nc.scalar, nc.sync)[quad % 2].dma_start(
+            nc.sync.dma_start(
                 out_2[0, 4 * quad : 4 * quad + 4, :].bitcast(I32), out_scales[32 * quad : 32 * quad + 4, :].bitcast(I32)
             )

@@ -92,6 +92,9 @@ def tile_list_msg_gelu_res_resLP_kernel(
         nc.gpsimd.memset(tab_sc[:].bitcast(I32), 0)
         wgo_rows = sbuf([P, P], F32, "wgo_rows")
         nc.vector.memset(wgo_rows[:], 0.0)
+        warm = sbuf([P, 16], F32, "warm")
+        nc.vector.memset(warm[:, 0:8], 0.0)
+        nc.scalar.activation(warm[:, 8:9], warm[:, 0:1], GELU)
         moved_sc = sbuf([P, 2 * J], U8, "moved_sc")
         nc.vector.memset(moved_sc[:].bitcast(I32), 0)
         ident = sbuf([P, P], F32, "ident")

@@ -36,16 +36,16 @@ EARLY_UNITS = (
 )
 KIB = 1024
 PLACED_AT = {
-    "w_raw0": 0, "sm_sb": 0, "wd8_sc": 64,
+    "w_grouped2": 0, "words1_512": 0,
     "words0_0": 8 * KIB, "w_codes0": 8 * KIB, "tab_sc": 12 * KIB, "r_sb0": 12 * KIB,
-    "w_raw1": 20 * KIB, "r_sb1": 20 * KIB, "h_codes0": 20 * KIB,
-    "w_raw2": 28 * KIB, "wd4": 28 * KIB, "wd8": 29 * KIB, "r_sb2": 31 * KIB, "act2": 31 * KIB, "act3": 31 * KIB,
-    "w_raw4": 39 * KIB, "parted1_512": 39 * KIB, "w_raw3": 43 * KIB, "words1_512": 43 * KIB, "r_sb3": 45 * KIB,
-    "h_codes1": 45 * KIB, "z0": 46 * KIB, "h_pairs2": 48 * KIB, "z1": 48 * KIB,
-    "h_pairs3": 53 * KIB, "z2": 53 * KIB, "h_grouped3": 55 * KIB, "z_late": 55 * KIB,
+    "w_raw0": 20 * KIB, "r_sb1": 20 * KIB, "h_codes0": 20 * KIB,
+    "w_raw1": 28 * KIB, "wd4": 28 * KIB, "wd8": 29 * KIB, "r_sb2": 31 * KIB, "act2": 31 * KIB, "act3": 31 * KIB,
+    "w_raw3": 39 * KIB, "parted1_512": 39 * KIB,
+    "w_raw2": 47 * KIB, "r_sb3": 47 * KIB, "h_codes1": 47 * KIB, "z0": 48 * KIB, "h_pairs2": 50 * KIB, "z1": 50 * KIB,
+    "h_pairs3": 55 * KIB, "z2": 55 * KIB, "h_grouped3": 57 * KIB, "z_late": 57 * KIB,
 }
 PAIRS_AT = 12 * KIB
-GROUPED_AT = 61 * KIB
+GROUPED_AT = 63 * KIB
 OUT_TILES = ((0, (512,)), (0, (384,)), (1, (512,)), (1, (256,)), (1, (256, 128)))
 OVERLAP = 8
 
@@ -81,11 +81,11 @@ def tile_list_msg_gelu_res_resLP_kernel(
         def pair_slot(pairs, t):
             return pairs[:].rearrange("p (u c e) -> p u c e", u=2, e=2)[:, t // 2, :, t % 2]
 
-        def load_scale_rows(plane, rows):
-            nc.gpsimd.memset(plane[:].bitcast(I32), 0)
-            for quad in range(QUADS):
+        def load_scale_rows(pieces):
+            for i, quad in [divmod(piece, QUADS) for piece in pieces]:
                 nc.sync.dma_start(
-                    plane[32 * quad : 32 * quad + 4, :].bitcast(I32), rows[0, 4 * quad : 4 * quad + 4, :].bitcast(I32)
+                    wd_sc[32 * quad : 32 * quad + 4, N * i : N * (i + 1)].bitcast(I32),
+                    (wd4_scales, wd8_scales)[i][0, 4 * quad : 4 * quad + 4, :].bitcast(I32),
                 )
 
         tab_sc = sbuf([P, T], U8, "tab_sc")
@@ -125,11 +125,11 @@ def tile_list_msg_gelu_res_resLP_kernel(
         load_weight(0, 0, R)
         nc.sync.dma_start(tab[:], tab_words[0].rearrange("p t i -> p (t i)").bitcast(I32))
         load_weight(1, 0, R)
-        wd4_sc = sbuf([P, N], U8, "wd4_sc")
-        load_scale_rows(wd4_sc, wd4_scales)
+        wd_sc = sbuf([P, 2 * N], U8, "wd_sc")
+        nc.gpsimd.memset(wd_sc[:].bitcast(I32), 0)
+        load_scale_rows(range(0, 5))
         load_weight(2, 0, R)
-        for c in range(2):
-            load_weight(3, R // 2 * c, R // 2)
+        load_weight(3, 0, R)
 
         wgo_col = sbuf([P, J // P], F32, "wgo_col")
         turned = bank([P, P], "wgo_turned", 2)
@@ -166,6 +166,19 @@ def tile_list_msg_gelu_res_resLP_kernel(
             nc.vector.tensor_copy(picked_sc[:, J * s : J * (s + 1)], tab_sc[:].indirect(lists[s][:]))
         early = [(s, 0, count, pick_words(s, 0, count)) for s, count in ((0, J), (1, HALF))]
         nc.sync.dma_start(moved_sc[0:MOVED_ROWS, :].bitcast(I32), picked_sc[16 : 16 + MOVED_ROWS, :].bitcast(I32))
+        r_rows = rT.rearrange("(p t) c -> p t c", t=PACK)
+        r_sb = []
+
+        def load_residual(n):
+            rows = sbuf([P, T], F32, "r_sb%d" % n)
+            nc.sync.dma_start(rows[:], r_rows[:, PACK - 1 - n, :])
+            r_sb.append(rows)
+
+        load_scale_rows([5])
+        load_residual(0)
+        load_scale_rows([6, 7])
+        sm_sb = sbuf([P, PACK], F32, "sm_sb")
+        nc.sync.dma_start(sm_sb[:], sm.rearrange("(p t) -> p t", t=PACK))
         for job in early:
             part_words(*job)
 
@@ -174,10 +187,7 @@ def tile_list_msg_gelu_res_resLP_kernel(
         def quantise_weight(i):
             grouped = sbuf([P, PACK * R], BF16, "w_grouped%d" % i)
             dealt = grouped[:].rearrange("p (t m j) -> p m j t", t=PACK, j=PACK)
-            raws = w_raw[i:] if i == 3 else w_raw[i : i + 1]
-            for c, raw in enumerate(raws):
-                part = P // len(raws)
-                nc.scalar.copy(dealt[:, part * c : part * (c + 1)], raw[:].rearrange("p j (m t) -> p m j t", t=PACK))
+            nc.scalar.copy(dealt, w_raw[i][:].rearrange("p j (m t) -> p m j t", t=PACK))
             codes = sbuf([P, R], U32, "w_codes%d" % i)
             scales = sbuf([P, R], U8, "w_scales%d" % i)
             nc.vector.quantize_mx(out=codes[:].bitcast(FP8X4), scales=scales[:], in_=grouped[:])
@@ -203,25 +213,12 @@ def tile_list_msg_gelu_res_resLP_kernel(
                 stop=(i == order[3] and u == 1),
             )
 
-        r_rows = rT.rearrange("(p t) c -> p t c", t=PACK)
-        r_sb = []
-
-        def load_residual(n):
-            rows = sbuf([P, T], F32, "r_sb%d" % n)
-            nc.sync.dma_start(rows[:], r_rows[:, PACK - 1 - n, :])
-            r_sb.append(rows)
-
         for i in range(4):
             quantise_weight(i)
             for t in range(PACK):
                 first_layer(0, t, i)
 
         part_words(1, HALF, HALF, pick_words(1, HALF, HALF))
-        load_residual(0)
-        wd8_sc = sbuf([P, N], U8, "wd8_sc")
-        load_scale_rows(wd8_sc, wd8_scales)
-        sm_sb = sbuf([P, PACK], F32, "sm_sb")
-        nc.sync.dma_start(sm_sb[:], sm.rearrange("(p t) -> p t", t=PACK))
         load_residual(1)
         wd4 = sbuf([P, 2 * N], U8, "wd4")
         wd8 = sbuf([P, N], I32, "wd8")
@@ -267,13 +264,13 @@ def tile_list_msg_gelu_res_resLP_kernel(
             for b in range(2):
                 cols = slice(P * b, P * (b + 1))
                 y_ps = bank([P, N], "y_ps%d%d" % (q, b), 2 + b)
-                for i, (packed, plane, fmt) in enumerate(((wd4, wd4_sc, FP4X4), (wd8, wd8_sc, FP8X4))):
+                for i, (packed, fmt) in enumerate(((wd4, FP4X4), (wd8, FP8X4))):
                     nc.tensor.matmul_mx(
                         out=y_ps[:],
                         lhsT=h_codes[q][:, cols].bitcast(FP8X4),
                         lhsT_scale=h_scales[q][:, cols],
                         rhs=packed[:].bitcast(fmt),
-                        rhs_scale=plane[:],
+                        rhs_scale=wd_sc[:, N * i : N * (i + 1)],
                         start=(i == 0),
                         stop=(i == 1),
                     )

@@ -102,28 +102,29 @@ def tile_list_msg_gelu_res_resLP_kernel(
 
         lists = [sbuf([P, J // PER_COL], U16, "list%d" % s) for s in range(2)]
         tab = sbuf([P, T], I32, "tab")
-        nc.sync.dma_start(lists[0][:], offs)
-        for r in range(4):
-            nc.sync.dma_start(
-                tab_sc[r:P:16, :].bitcast(I32),
-                tab_scales.rearrange("a (q r) c -> r q a c", r=4)[r].bitcast(I32),
-            )
-        nc.sync.dma_start(wgo_rows[0 : J // P, :], wgo[0].rearrange("(b c) -> b c", c=P))
-        nc.sync.dma_start(lists[1][:], offs2)
 
         def weight_rows(i):
             a, s = divmod(i, 2)
             return (ws, wt)[s][K_PASS * a : K_PASS * (a + 1), :].rearrange("(p j) r -> p j r", j=PACK)
 
-        w_raw = []
+        w_raw = [sbuf([P, PACK, R], F32, "w_raw0")]
+        nc.sync.dma_start(lists[0][:], offs)
+        nc.sync.dma_start(w_raw[0][:, 0, :], weight_rows(0)[:, 0, :])
+        for r in range(4):
+            nc.sync.dma_start(
+                tab_sc[r:P:16, :].bitcast(I32),
+                tab_scales.rearrange("a (q r) c -> r q a c", r=4)[r].bitcast(I32),
+            )
+        nc.sync.dma_start(lists[1][:], offs2)
+        nc.sync.dma_start(w_raw[0][:, 1:PACK, :], weight_rows(0)[:, 1:PACK, :])
+        nc.sync.dma_start(wgo_rows[0 : J // P, :], wgo[0].rearrange("(b c) -> b c", c=P))
+        nc.sync.dma_start(tab[:], tab_words[0].rearrange("p t i -> p (t i)").bitcast(I32))
 
         def load_weight(i, first, count):
             raw = sbuf([P, PACK, count], F32, "w_raw%d" % len(w_raw))
             nc.sync.dma_start(raw[:], weight_rows(i)[:, :, first : first + count])
             w_raw.append(raw)
 
-        load_weight(0, 0, R)
-        nc.sync.dma_start(tab[:], tab_words[0].rearrange("p t i -> p (t i)").bitcast(I32))
         load_weight(1, 0, R)
         wd_sc = sbuf([P, 2 * N], U8, "wd_sc")
         nc.gpsimd.memset(wd_sc[:].bitcast(I32), 0)
@@ -134,15 +135,13 @@ def tile_list_msg_gelu_res_resLP_kernel(
         wgo_col = sbuf([P, J // P], F32, "wgo_col")
         turned = bank([P, P], "wgo_turned", 2)
         nc.tensor.transpose(turned[:], wgo_rows[:], ident[:])
-        to_spread = sbuf([P, J // P], F32, "to_spread", "w_grouped0")
-        nc.scalar.copy(to_spread[:], turned[:, 0 : J // P])
         nc.scalar.copy(wgo_col[:], turned[:, 0 : J // P])
         wgo_sb = sbuf([P, J], F32, "wgo_sb")
         for g in range(2):
             spread = bank([P, PACK, P], "wgo_spread%d" % g, 6 + g)
             for b in range(PACK):
                 col = PACK * g + b
-                nc.tensor.transpose(spread[:, b, :], to_spread[:, col : col + 1].to_broadcast([P, P]), ident[:])
+                nc.tensor.transpose(spread[:, b, :], wgo_col[:, col : col + 1].to_broadcast([P, P]), ident[:])
             nc.scalar.copy(wgo_sb[:, HALF * g : HALF * (g + 1)], spread[:].rearrange("p b c -> p (b c)"))
 
         picked_sc = sbuf([P, 2 * J], U8, "picked_sc")

from contextlib import ExitStack

import concourse.mybir as mybir
from concourse.masks import make_identity

K, R, N, T, J = 1024, 512, 512, 2048, 1024
FLOPS = 2 * J * (2 * K * R + 2 * R * N)

F32 = mybir.dt.float32
BF16 = mybir.dt.bfloat16
I32 = mybir.dt.int32
U32 = mybir.dt.uint32
U16 = mybir.dt.uint16
U8 = mybir.dt.uint8
FP8X4 = mybir.dt.float8_e4m3fn_x4
FP4X4 = mybir.dt.float4_e2m1fn_x4
MULT = mybir.AluOpType.mult
ADD = mybir.AluOpType.add
GELU = mybir.ActivationFunctionType.Gelu_apprx_tanh
COPY = mybir.ActivationFunctionType.Copy

P = 128
PACK = 4
K_PASS = P * PACK
QUADS = 4
HALF = J // 2
QUARTER = J // 4
PER_COL = 16
MOVED_ROWS = 112
PASS_ORDER = ((0, 1, 2, 3), (3, 2, 1, 0))
EARLY_UNITS = (
    [[(1, 0, 2), (2, 0, 2)]],
    [[(3, 0, 2)], [(0, 2, 2), (1, 2, 2)]],
    [[(0, 4, 2)], [(1, 4, 2)]],
    [[(0, 6, 1), (1, 6, 1)], [(0, 7, 1), (1, 7, 1)]],
)
KIB = 1024
PLACED_AT = {
    "w_grouped2": 0, "words1_512": 0,
    "words0_0": 8 * KIB, "w_codes0": 8 * KIB, "tab_sc": 12 * KIB, "r_sb0": 12 * KIB,
    "w_raw0": 20 * KIB, "r_sb1": 20 * KIB, "h_codes0": 20 * KIB,
    "w_raw1": 28 * KIB, "wd4": 28 * KIB, "wd8": 29 * KIB, "r_sb2": 31 * KIB, "act2": 31 * KIB, "act3": 31 * KIB,
    "w_raw3": 39 * KIB, "parted1_512": 39 * KIB,
    "w_raw2": 47 * KIB, "r_sb3": 47 * KIB, "h_codes1": 47 * KIB, "z0": 48 * KIB, "h_pairs2": 50 * KIB, "z1": 50 * KIB,
    "h_pairs3": 55 * KIB, "z2": 55 * KIB, "h_grouped3": 57 * KIB, "z_late": 57 * KIB,
}
PAIRS_AT = 12 * KIB
GROUPED_AT = 63 * KIB
OUT_TILES = ((0, (512,)), (0, (384,)), (1, (512,)), (1, (256,)), (1, (256, 128)))
OVERLAP = 8


def tile_list_msg_gelu_res_resLP_kernel(
    tc, tab_words, tab_scales, ws, wt, sm, wd4_words, wd4_scales, wd8_words, wd8_scales, rT, wgo, offs, offs2,
    out_0, out_1, out_2,
):
    nc = tc.nc
    with ExitStack() as ctx:
        sb = ctx.enter_context(tc.tile_pool(name="sb", bufs=1))
        placed = ctx.enter_context(tc.tile_pool(name="placed", bufs=1))
        ps = ctx.enter_context(tc.psum_pool(name="ps", bufs=1))

        def sbuf(shape, dtype, name, slot=None, at=None):
            at = PLACED_AT.get(name, at)
            if at is not None:
                return placed.tile(shape, dtype, name=name, offset=at, align_bytes=64)
            return sb.tile(shape, dtype, name=name, tag=slot or name, align_bytes=64)

        def bank(shape, name, index):
            return ps.tile(shape, F32, name=name, tag="bank%d" % index)

        def entries(list_tile, first, count):
            return list_tile[:, first // PER_COL : (first + count) // PER_COL]

        def weave_words(copy, dtype, grouped, pairs):
            copy(
                grouped[:].bitcast(dtype).rearrange("p (c u) -> p c u", u=2),
                pairs[:].bitcast(dtype).rearrange("p (u c) -> p c u", u=2),
            )

        def pair_slot(pairs, t):
            return pairs[:].rearrange("p (u c e) -> p u c e", u=2, e=2)[:, t // 2, :, t % 2]

        def load_scale_rows(pieces):
            for i, quad in [divmod(piece, QUADS) for piece in pieces]:
                nc.sync.dma_start(
                    wd_sc[32 * quad : 32 * quad + 4, N * i : N * (i + 1)].bitcast(I32),
                    (wd4_scales, wd8_scales)[i][0, 4 * quad : 4 * quad + 4, :].bitcast(I32),
                )

        tab_sc = sbuf([P, T], U8, "tab_sc")
        nc.gpsimd.memset(tab_sc[:].bitcast(I32), 0)
        wgo_rows = sbuf([P, P], F32, "wgo_rows")
        nc.vector.memset(wgo_rows[:], 0.0)
        warm = sbuf([P, 16], F32, "warm")
        nc.vector.memset(warm[:, 0:8], 0.0)
        nc.scalar.activation(warm[:, 8:9], warm[:, 0:1], GELU)
        moved_sc = sbuf([P, 2 * J], U8, "moved_sc")
        nc.vector.memset(moved_sc[:].bitcast(I32), 0)
        ident = sbuf([P, P], F32, "ident")
        make_identity(nc, ident[:])

        lists = [sbuf([P, J // PER_COL], U16, "list%d" % s) for s in range(2)]
        tab = sbuf([P, T], I32, "tab")

        def weight_rows(i):
            a, s = divmod(i, 2)
            return (ws, wt)[s][K_PASS * a : K_PASS * (a + 1), :].rearrange("(p j) r -> p j r", j=PACK)

        w_raw = [sbuf([P, PACK, R], F32, "w_raw0")]
        nc.sync.dma_start(lists[0][:], offs)
        nc.sync.dma_start(w_raw[0][:, 0, :], weight_rows(0)[:, 0, :])
        for r in range(4):
            nc.sync.dma_start(
                tab_sc[r:P:16, :].bitcast(I32),
                tab_scales.rearrange("a (q r) c -> r q a c", r=4)[r].bitcast(I32),
            )
        nc.sync.dma_start(lists[1][:], offs2)
        nc.sync.dma_start(w_raw[0][:, 1:PACK, :], weight_rows(0)[:, 1:PACK, :])
        nc.sync.dma_start(wgo_rows[0 : J // P, :], wgo[0].rearrange("(b c) -> b c", c=P))
        nc.sync.dma_start(tab[:], tab_words[0].rearrange("p t i -> p (t i)").bitcast(I32))

        def load_weight(i, first, count):
            raw = sbuf([P, PACK, count], F32, "w_raw%d" % len(w_raw))
            nc.sync.dma_start(raw[:], weight_rows(i)[:, :, first : first + count])
            w_raw.append(raw)

        load_weight(1, 0, R)
        wd_sc = sbuf([P, 2 * N], U8, "wd_sc")
        nc.gpsimd.memset(wd_sc[:].bitcast(I32), 0)
        load_scale_rows(range(0, 5))
        load_weight(2, 0, R)
        load_weight(3, 0, R)

        wgo_col = sbuf([P, J // P], F32, "wgo_col")
        turned = bank([P, P], "wgo_turned", 2)
        nc.tensor.transpose(turned[:], wgo_rows[:], ident[:])
        nc.scalar.copy(wgo_col[:], turned[:, 0 : J // P])
        wgo_sb = sbuf([P, J], F32, "wgo_sb")
        for g in range(2):
            spread = bank([P, PACK, P], "wgo_spread%d" % g, 6 + g)
            for b in range(PACK):
                col = PACK * g + b
                nc.tensor.transpose(spread[:, b, :], wgo_col[:, col : col + 1].to_broadcast([P, P]), ident[:])
            nc.scalar.copy(wgo_sb[:, HALF * g : HALF * (g + 1)], spread[:].rearrange("p b c -> p (b c)"))

        picked_sc = sbuf([P, 2 * J], U8, "picked_sc")
        parted = {}

        def pick_words(s, first, count):
            words = sbuf([P, count], U32, "words%d_%d" % (s, first))
            nc.vector.tensor_copy(words[:], tab[:].bitcast(U32).indirect(entries(lists[s], first, count)))
            return words

        def part_words(s, first, count, words):
            both = sbuf([P, 2, 2 * count], U8, "parted%d_%d" % (s, first))
            nc.vector.tensor_copy(
                both[:].rearrange("p d b -> p (d b)").bitcast(U16).rearrange("p (d j) -> p d j", d=2),
                words[:].bitcast(U16).rearrange("p (j d) -> p d j", d=2),
            )
            for q in range(first // QUARTER, (first + count) // QUARTER):
                parted[s, q] = both[:, :, 2 * (QUARTER * q - first) : 2 * (QUARTER * (q + 1) - first)]

        for s in range(2):
            nc.vector.tensor_copy(picked_sc[:, J * s : J * (s + 1)], tab_sc[:].indirect(lists[s][:]))
        early = [(s, 0, count, pick_words(s, 0, count)) for s, count in ((0, J), (1, HALF))]
        nc.sync.dma_start(moved_sc[0:MOVED_ROWS, :].bitcast(I32), picked_sc[16 : 16 + MOVED_ROWS, :].bitcast(I32))
        r_rows = rT.rearrange("(p t) c -> p t c", t=PACK)
        r_sb = []

        def load_residual(n):
            rows = sbuf([P, T], F32, "r_sb%d" % n)
            nc.sync.dma_start(rows[:], r_rows[:, PACK - 1 - n, :])
            r_sb.append(rows)

        load_scale_rows([5])
        load_residual(0)
        load_scale_rows([6, 7])
        sm_sb = sbuf([P, PACK], F32, "sm_sb")
        nc.sync.dma_start(sm_sb[:], sm.rearrange("(p t) -> p t", t=PACK))
        for job in early:
            part_words(*job)

        w_codes, w_scales = [], []

        def quantise_weight(i):
            grouped = sbuf([P, PACK * R], BF16, "w_grouped%d" % i)
            dealt = grouped[:].rearrange("p (t m j) -> p m j t", t=PACK, j=PACK)
            nc.scalar.copy(dealt, w_raw[i][:].rearrange("p j (m t) -> p m j t", t=PACK))
            codes = sbuf([P, R], U32, "w_codes%d" % i)
            scales = sbuf([P, R], U8, "w_scales%d" % i)
            nc.vector.quantize_mx(out=codes[:].bitcast(FP8X4), scales=scales[:], in_=grouped[:])
            w_codes.append(codes)
            w_scales.append(scales)

        acc = {}

        def first_layer(q, t, i):
            a, s = divmod(i, 2)
            b, u = divmod(t, 2)
            order = PASS_ORDER[min(q, 1)]
            if i == order[0] and u == 0:
                acc[q, b] = bank([P, 2, QUARTER], "acc%d%d" % (q, b), 6 * (q % 2) + b)
            first = J * s + QUARTER * q
            nc.tensor.matmul_mx(
                out=acc[q, b][:, u, :],
                lhsT=w_codes[i][:, P * t : P * (t + 1)].bitcast(FP8X4),
                lhsT_scale=w_scales[i][:, P * t : P * (t + 1)],
                rhs=parted[s, q][:, a, :].bitcast(FP4X4),
                rhs_scale=(picked_sc, moved_sc)[a][:, first : first + QUARTER],
                start=(i == order[0] and u == 0),
                stop=(i == order[3] and u == 1),
            )

        for i in range(4):
            quantise_weight(i)
            for t in range(PACK):
                first_layer(0, t, i)

        part_words(1, HALF, HALF, pick_words(1, HALF, HALF))
        load_residual(1)
        wd4 = sbuf([P, 2 * N], U8, "wd4")
        wd8 = sbuf([P, N], I32, "wd8")
        nc.sync.dma_start(wd4[:].bitcast(I32), wd4_words[0].bitcast(I32))
        nc.sync.dma_start(wd8[:], wd8_words[0].rearrange("p n i -> p (n i)").bitcast(I32))
        load_residual(2)
        load_residual(3)

        page = [sbuf([P, T], F32, "page%d" % t) for t in range(PACK)]
        for t in range(PACK):
            for c in range(0, T, T // 4):
                nc.gpsimd.memset(page[t][:, c : c + T // 4], 0.0)

        rw = {}

        def pick_residual(n):
            t = PACK - 1 - n
            rw[t] = sbuf([P, J], F32, "rw%d" % t)
            nc.vector.tensor_tensor(rw[t][:], r_sb[n][:].indirect(lists[1][:]), wgo_sb[:], MULT)

        act, h_codes, h_scales, y_sb = {}, {}, {}, {}

        def gelu(q):
            if q > 0:
                for t in range(PACK):
                    for i in PASS_ORDER[1]:
                        first_layer(q, t, i)
            act[q] = sbuf([P, PACK, QUARTER], F32, "act%d" % q, "act")
            for b in range(2):
                nc.scalar.activation(act[q][:, 2 * b : 2 * b + 2, :], acc[q, b][:], GELU)

        def hidden(q):
            pairs = sbuf([P, PACK * QUARTER], BF16, "h_pairs%d" % q)
            for t in range(PACK):
                nc.scalar.activation(pair_slot(pairs, t), act[q][:, t, :], COPY, scale=sm_sb[:, t : t + 1])
            grouped = sbuf([P, PACK * QUARTER], BF16, "h_grouped%d" % q)
            weave_words(nc.scalar.copy, U32, grouped, pairs)
            h_codes[q] = sbuf([P, QUARTER], U32, "h_codes%d" % q)
            h_scales[q] = sbuf([P, QUARTER], U8, "h_scales%d" % q)
            nc.vector.quantize_mx(out=h_codes[q][:].bitcast(FP8X4), scales=h_scales[q][:], in_=grouped[:])

        def second_layer(q):
            for b in range(2):
                cols = slice(P * b, P * (b + 1))
                y_ps = bank([P, N], "y_ps%d%d" % (q, b), 2 + b)
                for i, (packed, fmt) in enumerate(((wd4, FP4X4), (wd8, FP8X4))):
                    nc.tensor.matmul_mx(
                        out=y_ps[:],
                        lhsT=h_codes[q][:, cols].bitcast(FP8X4),
                        lhsT_scale=h_scales[q][:, cols],
                        rhs=packed[:].bitcast(fmt),
                        rhs_scale=wd_sc[:, N * i : N * (i + 1)],
                        start=(i == 0),
                        stop=(i == 1),
                    )
                y_sb[q, b] = sbuf([P, PACK, P], F32, "y_sb%d%d" % (q, b))
                block = 2 * q + b
                nc.scalar.activation(
                    y_sb[q, b][:],
                    y_ps[:].rearrange("j (p t) -> j t p", t=PACK),
                    COPY,
                    scale=wgo_col[:, block : block + 1],
                )

        def turn(z, place, units, index):
            width = P * sum(unit[2] for unit in units)
            z_ps = bank([P, width], "z_ps%d%d" % units[0][0:2], index)
            first = 0
            for t, first_block, blocks in units:
                for block in range(first_block, first_block + blocks):
                    nc.tensor.transpose(z_ps[:, first : first + P], y_sb[divmod(block, 2)][:, t, :], ident[:])
                    first = first + P
            nc.scalar.copy(z[:, place : place + width], z_ps[:])

        def scatter(t, first_block, blocks, z):
            first, count = P * first_block, P * blocks
            nc.vector.tensor_tensor(
                page[t][:].indirect(entries(lists[1], first, count)), z, rw[t][:, first : first + count], ADD
            )

        def place(name, groups):
            z = sbuf([P, P * sum(unit[2] for group in groups for unit in group)], F32, name)
            first = 0
            for n, group in enumerate(groups):
                turn(z, first, group, 4 + n % 2)
                for unit in group:
                    scatter(*unit, z[:, first : first + P * unit[2]])
                    first = first + P * unit[2]

        pick_residual(0)
        pick_residual(1)
        gelu(0)
        hidden(0)
        pick_residual(2)
        pick_residual(3)
        for q in range(4):
            if q < 3:
                gelu(q + 1)
            second_layer(q)
            if q < 3:
                hidden(q + 1)
            if q == 0:
                place("z_first", [[(0, 0, 2)]])
            place("z%d" % q, EARLY_UNITS[q])
        z_late = sbuf([P, 2, 3 * QUARTER], F32, "z_late")
        for e in range(2):
            turn(z_late[:, e, :], 0, [(2 + e, 2, 4)], e)
            turn(z_late[:, e, :], HALF, [(2 + e, 6, 2)], 6 + e)
            scatter(2 + e, 2, 6, z_late[:, e, :])

        out_rows = out_0.rearrange("(p t) c -> p t c", t=PACK)
        tiles = []
        for n, (side, widths) in enumerate(OUT_TILES):
            start = sum(sum(w) for s, w in OUT_TILES[:n])
            pairs = sbuf([P, PACK * sum(widths)], BF16, "out_pairs%d" % n, at=PAIRS_AT + 2 * PACK * start)
            tiles.append((start, side, widths, pairs))
        for t in range(PACK):
            nc.sync.dma_start(out_rows[:, t, :], page[t][:])
            for start, side, widths, pairs in tiles:
                width = sum(widths)
                if side == 0 and t == 2:
                    whole = width - OVERLAP
                    nc.scalar.copy(pair_slot(pairs, t)[:, 0:whole], page[t][:, start : start + whole])
                    nc.scalar.copy(
                        pairs[:].rearrange("p (u c e) -> p u c e", u=2, e=2)[:, 1, whole:width, :],
                        page[t][:, start + whole : start + width].unsqueeze(2).to_broadcast([P, OVERLAP, 2]),
                    )
                else:
                    copy = nc.vector.tensor_copy if (t == 3 and side == 0) else nc.scalar.copy
                    copy(pair_slot(pairs, t), page[t][:, start : start + width])
        out_codes = sbuf([P, T], I32, "out_codes")
        out_scales = sbuf([P, T], U8, "out_scales")
        words_out = out_1[0].rearrange("p t i -> p (t i)").bitcast(I32)
        pieces = []
        for start, side, widths, pairs in tiles:
            copy, dtype = ((nc.vector.tensor_copy, I32), (nc.scalar.copy, U32))[side]
            first = 0
            for width in widths:
                at = GROUPED_AT + 2 * PACK * (start + first)
                grouped = sbuf([P, PACK * width], BF16, "out_grouped%d" % len(pieces), at=at)
                copy(
                    grouped[:].bitcast(dtype).rearrange("p (c u) -> p c u", u=2),
                    pairs[:].bitcast(dtype).rearrange("p (u c) -> p c u", u=2)[:, first : first + width, :],
                )
                pieces.append((slice(start + first, start + first + width), grouped))
                first = first + width
        for cols, grouped in pieces:
            nc.vector.quantize_mx(out=out_codes[:, cols].bitcast(FP8X4), scales=out_scales[:, cols], in_=grouped[:])
            nc.sync.dma_start(words_out[:, cols], out_codes[:, cols])
        for quad in range(QUADS):
            nc.sync.dma_start(
                out_2[0, 4 * quad : 4 * quad + 4, :].bitcast(I32), out_scales[32 * quad : 32 * quad + 4, :].bitcast(I32)
            )
